import numpy as np, ml_dtypes
CORES = [5,29,101,125,133,157,229,253]
N = 8
BF = ml_dtypes.bfloat16
def gentries(a):
    return np.ascontiguousarray(a.reshape(8, 16, -1).transpose(0, 2, 1)).reshape(8, -1)
def gtable(e):
    e = np.asarray(e); return np.ascontiguousarray(e.reshape(8, -1, 16).transpose(0, 2, 1)).reshape(128, -1).astype(np.int32)
TT, P, R, S, CAP = 1024, 384, 2, 3, 16
def walk(planes, nbr, x, c):
    A = planes.astype(np.int64).reshape(N, 4, 4, TT).transpose(0, 3, 1, 2).reshape(N * TT, 4, 4); B = nbr.astype(np.int64).transpose(0, 2, 1).reshape(N * TT, 4)
    h = np.concatenate([x.astype(np.int64), np.ones((len(x), 1), np.int64)], 1); c = c.astype(np.int64); w = [c]
    for k in range(R):
        q = c // TT
        for s in range(S):
            v = np.einsum("mfc,mc->mf", A[c], h); face = np.argmin(v, 1)
            c = np.where((c // TT == q) & (np.min(v, 1) < 0), B[c, face], c)
        w.append(c)
    return np.stack(w)
def codes(rng, shape, own):
    r = np.arange(N).reshape(N, 1, 1); q = np.where(rng.random(shape) < own, r, (r + rng.integers(1, N, shape)) % N)
    return q * TT + rng.integers(0, TT, shape)
def mesh(rng, big, lo, hi):
    p = rng.integers(-big, big + 1, (N, 4, 4, TT)); p[:, :, 3] = rng.integers(lo, hi + 1, (N, 4, TT)); return p
def roomy(rng, p):
    h = np.stack([1 + rng.permutation(TT - 2)[:TT // 16] for r in range(N)]); k = h.shape[1]
    for r in range(N):
        u = p[r]; u[:, :3, h[r]] = rng.integers(-255, 256, (4, 3, k)); u[:, 3, h[r]] = rng.integers(3 * 255 * 1023, 2 ** 20 + 1, (4, k))
    return h
def choose(rng, p, h, b, x, c):
    big = int(np.abs(x).max()); r = np.arange(N).reshape(N, 1, 1)
    x = np.concatenate([x, rng.integers(-big, big + 1, (N, 8, P, 3))], 2); c = np.concatenate([c, r * TT + h[r, rng.integers(0, h.shape[1], (N, 8, P))]], 2)
    planes = p.reshape(N, 16, TT).astype(np.int32); m = c.shape[2]
    w = walk(planes, b, x.reshape(-1, 3), c.reshape(-1))[:R].reshape(R, N, 8, m) // TT
    cap = np.where(np.eye(N, dtype=bool), P, CAP); cnt = np.zeros((R, N, 8, N), np.int64); n = np.zeros((N, 8), np.int64); keep = np.zeros((N, 8, m), bool)
    k, i, g = np.ogrid[:R, :N, :8]
    for j in range(m):
        q = w[:, :, :, j]; ok = np.all(cnt[k, i, g, q] < cap[i, q], axis=0) & (n < P)
        cnt[k, i, g, q] += ok; n += ok; keep[:, :, j] = ok
    e = rng.permuted(np.nonzero(keep.reshape(N * 8, m))[1].reshape(N, 8, P), axis=2)
    x = np.take_along_axis(x, e[:, :, :, None], 2); c = np.take_along_axis(c, e, 2)
    return {"planes": planes, "nbr": b.astype(np.int32), "pts": np.ascontiguousarray(x.transpose(0, 1, 3, 2)).reshape(N, 24, P).astype(np.int32), "tet0": np.stack([gtable(u) for u in c])}
def setup_inputs(rng):
    p = mesh(rng, 127, -20000, 60000); h = roomy(rng, p)
    return choose(rng, p, h, codes(rng, (N, 4, TT), 0.6), rng.integers(-255, 256, (N, 8, 3 * P, 3)), codes(rng, (N, 8, 3 * P), 0.5))
def setup_inputs_full(rng):
    p = mesh(rng, 127, -20000, 60000); h = roomy(rng, p); r = np.arange(N).reshape(N, 1, 1); m = (N - 1) * CAP
    q = np.broadcast_to((r + 1 + np.arange(m) // CAP) % N, (N, 8, m)); c = q * TT + h[q, rng.integers(0, h.shape[1], (N, 8, m))]
    c = np.where(np.arange(8).reshape(1, 8, 1) % 2 == 0, c, codes(rng, (N, 8, m), 0.0)); c = np.concatenate([c, codes(rng, (N, 8, 2 * P), 0.8)], 2)
    return choose(rng, p, h, codes(rng, (N, 4, TT), 0.6), rng.integers(-255, 256, (N, 8, m + 2 * P, 3)), c)
def setup_inputs_ties(rng):
    p = mesh(rng, 1, -1, 2)
    p[:, 3] = np.where(rng.random((N, 1, TT)) < 0.5, p[:, 1], p[:, 3]); p[:, 2] = np.where(rng.random((N, 1, TT)) < 0.5, p[:, 0], p[:, 2]); h = roomy(rng, p)
    return choose(rng, p, h, codes(rng, (N, 4, TT), 0.6), rng.integers(-2, 3, (N, 8, 3 * P, 3)), codes(rng, (N, 8, 3 * P), 0.5))
def setup_inputs_few(rng):
    p = mesh(rng, 127, -20000, 60000); h = roomy(rng, p); b = codes(rng, (N, 4, TT), 1.0); q = rng.integers(0, N); b[q] = codes(rng, (N, 4, TT), 0.3)[q]
    c = codes(rng, (N, 8, 3 * P), 1.0); out = []
    for v in (b, c):
        u = rng.random(v.shape); out.append(np.where(u < 0.2, v // TT * TT, np.where(u < 0.4, v // TT * TT + TT - 1, v)))
    b, c = out; x = rng.integers(-255, 256, (N, 8, 3 * P, 3)); one = rng.random((N, 8, 3 * P)) < 0.4
    c = np.where(one, c[:, :, :1], c); x = np.where(one[:, :, :, None], x[:, :, :1], x)
    return choose(rng, p, h, b, x, c)
def setup_inputs_spread(rng):
    def some(bits, top, shape, plus):
        v = np.minimum(np.floor(np.exp2(bits * rng.random(shape))).astype(np.int64), top); v = np.where(rng.random(shape) < 0.125, top, v)
        return np.where(rng.random(shape) < plus, v, -v)
    p = some(10, 1023, (N, 4, 4, TT), 0.5); p[:, :, 3] = some(20, 2 ** 20, (N, 4, TT), 0.75); h = roomy(rng, p)
    return choose(rng, p, h, codes(rng, (N, 4, TT), 0.6), some(10, 1023, (N, 8, 3 * P, 3), 0.5), codes(rng, (N, 8, 3 * P), 0.5))
def points(pts, tet0):
    return pts.reshape(N, 8, 3, P).transpose(0, 1, 3, 2).reshape(-1, 3), np.stack([gentries(a) for a in tet0]).reshape(-1)
def check_inputs(d):
    bad = []; p = d["planes"].astype(np.int64).reshape(N, 4, 4, TT)
    if np.abs(p[:, :, :3]).max() > 1023 or np.abs(p[:, :, 3]).max() > 2 ** 20: bad.append("planes out of range")
    if np.abs(d["pts"].astype(np.int64)).max() > 1023: bad.append("pts out of range")
    for a in ("nbr", "tet0"):
        if d[a].min() < 0 or d[a].max() >= N * TT: bad.append(a + " out of range")
    if bad: return bad
    x, c = points(d["pts"], d["tet0"]); w = walk(d["planes"], d["nbr"], x, c)[:R].reshape(R, N, 8, P) // TT
    for q in range(N):
        n = np.count_nonzero(w == q, axis=3); n[:, q] = 0
        if n.max() > CAP: bad.append("more than CAP points of a group on rank " + str(q))
    return bad
def reference(planes, nbr, pts, tet0):
    x, c = points(pts, tet0); e = walk(planes, nbr, x, c)[R].reshape(N, 8, P)
    return {"y": np.stack([gtable(u) for u in e]).astype(np.float32)}

@@ -1,0 +1,589 @@
+from concourse.bass import DstId, RemoteDMATransfer
+from concourse.mybir import AluOpType as A, ActivationFunctionType as F
+
+NT, NP, NK = 1024, 384, 24
+LO, HI, PWID = 8, 1032, 1040
+DEAD = 7.375
+MSG = 17
+WIN = 640
+BIG = 8388608.0
+N_REL, ENG_HOP, ENG_OUT, ENG_DIR = 2, 4, 4, 2
+PER = 4 // N_REL
+
+_sb = {
+    "X": ([128, NP], "int32"), "L0": ([128, NK], "int32"), "PW": ([128, PWID], "int32"), "NB": ([128, PWID], "int32"),
+    "ND": ([128, PWID], "float32"), "Xv": ([128, 112], "float32"), "xB": ([128, 112], "float32"),
+    "pi": ([128, 4], "int32"), "pj": ([128, 8], "int32"), "pf": ([128, 4], "float32"), "jm": ([128, NP], "float32"),
+    "mk": ([128, 128], "float32"), "md16": ([128, 128], "float32"), "m16": ([128, NP], "float32"), "Rd": ([128, NP], "float32"),
+    "G16": ([128, 128], "float16"), "G2k": ([128, 128], "float16"), "Gf": ([128, 128], "float32"),
+    "U16": ([128, 128], "float16"), "I16": ([128, 128], "float16"), "If": ([128, 128], "float32"),
+    "S1": ([128, 40], "float32"), "S2": ([128, 40], "float32"), "sC": ([128, 40], "float32"), "Ms": ([128, 8], "float32"),
+    "K0": ([128, 120], "float32"), "R1c": ([128, 120], "float32"),
+    "oKi": ([128, NK], "int32"), "oRi": ([128, 12], "float32"), "oT": ([128, 72], "uint16"),
+    "Rs": ([128, 224], "float32"), "cQ": ([128, 256], "float32"), "cD": ([128, 224], "bfloat16"), "bc": ([128, 512], "bfloat16"),
+    "cOw": ([128, NK], "float32"), "cO16": ([128, NK], "float16"), "cS": ([128, 8], "float32"),
+    "rk": ([128, 48], "int32"), "ci": ([128, NK], "int32"), "ti": ([128, NK], "int32"), "rkB": ([128, 8], "int32"),
+    "oh1": ([128, 192], "float16"), "ohA": ([128, 192], "float16"), "ex": ([128, NP], "float16"), "scn": ([128, 168], "float32"),
+    "z1": ([128, 168], "float16"), "z2": ([128, 192], "float16"), "cnt": ([128, 8], "float16"), "PK": ([128, NP], "int32"),
+    "su1": ([128, NK], "uint16"), "suA": ([128, NK], "uint16"), "suB": ([128, 8], "uint16"),
+    "W1": ([128, WIN], "int32"), "W2": ([128, WIN], "int32"),
+    "dg": ([128, 112], "float32"), "sd": ([128, 112], "int32"), "yi1": ([128, 112], "int32"), "yi2": ([128, 112], "int32"),
+    "tl1": ([128, 8], "int32"), "tl2": ([128, 8], "int32"),
+    "msg1": ([128, 7, MSG], "float16"), "msg2": ([128, 7, MSG], "float16"),
+    "land1": ([128, 7, MSG], "float16"), "land2": ([128, 7, MSG], "float16"),
+    "sBv": ([128, 8], "float32"), "sBg": ([128, 8], "float32"),
+    "out1": ([128, 8], "float32"), "out2": ([128, 8], "float32"), "rep1": ([128, 8], "float32"), "rep2": ([128, 8], "float32"),
+    "Lo": ([128, NK], "float32"), "wO": ([128, NK], "uint16"), "Lv": ([128, 8], "float32"), "Lv0": ([128, 8], "float32"),
+    "Ld": ([128, 8], "float32"), "wv": ([128, 8], "uint16"), "Lb": ([128, 8], "float32"), "wr": ([128, 8], "uint16"),
+    "smA": ([128, NK], "float32"), "smB": ([128, 8], "float32"), "vB": ([128, 8], "float32"), "exv": ([128, 112], "float32"),
+    "vW": ([128, 120], "float32"), "s1c": ([128, NK], "uint16"), "gv": ([128, NP], "float32"), "sv": ([128, NP], "float32"),
+    "vO": ([128, NK], "float32"), "vt": ([128, NK], "int32"), "tau": ([128, NK], "uint16"),
+    "Yb": ([128, NK], "float32"), "dW": ([128, 136], "float32"),
+    "hq1": ([128, PER, MSG], "float16"), "hq2": ([128, PER, MSG], "float16"), "hp1": ([128, PER], "float32"), "hp2": ([128, PER], "float32"),
+}
+for _t, _n in (("O", 384), ("V", 128), ("R", 128)):
+    _m = _n // 128 * 40
+    for _b, _w in (("pr", _n), ("pa", _n), ("u", _m + 8), ("c", _m), ("k", _m), ("p", _m), ("re", _m), ("e", _n)):
+        _sb[_b + _t] = ([128, _w], "float32")
+SCRATCH = {_k: ("sbuf", _v[0], _v[1]) for _k, _v in _sb.items()}
+PSUM = ("oK", "oP", "vK", "vP", "vL", "rA", "rB", "rC")
+for _k in PSUM:
+    SCRATCH[_k] = ("psum", [128, 512], "float32")
+SEMAPHORES = ["sV", "sS", "sT", "sG", "ldA", "ldP", "ldB", "ldC", "st", "rq1", "rq2", "rp1", "rp2", "hq1", "hq2", "hp1", "hp2", "loc"]
+
+FLY_REQ, FLY_REP = 6.5, 6.5
+WAKE, SLACK, SLACK2 = 0.06, 0.1, 0.2
+P_O1, P_O2, P_A, P_O3, P_R, P_C = 3, 2, 2, 5, 4, 4
+
+
+def wiring(T, topo, core):
+    others = [c for c in T.cores if c != core]
+    cross = [c for c in others if not topo.may_write(core, c)]
+    direct = [c for c in others if topo.may_write(core, c)]
+    rel = [c for c in topo.cores_of(core) if c not in T.cores and all(topo.may_write(c, d) for d in cross)]
+    rel.sort(key=lambda c: (topo.die(c) != topo.die(core), c))
+    return cross, direct, rel[:N_REL]
+
+
+def emask(engs):
+    return sum(1 << e for e in engs)
+
+
+def place_of(T, topo, owner, dst):
+    cross, direct, rel = wiring(T, topo, dst)
+    return (cross + direct).index(owner)
+
+
+def relay_program(g, core, T, topo, owner):
+    cross, direct, rel = wiring(T, topo, owner)
+    k = rel.index(core)
+    dsts = cross[PER * k:PER * k + PER]
+    n = 0
+    for src, dname, sem_out, req in (("hq1", "land1", "rq1", True), ("hp1", "rep1", "rp1", False),
+                                     ("hq2", "land2", "rq2", True), ("hp2", "rep2", "rp2", False)):
+        g.wait_ge(T.sem[src], ENG_HOP)
+        trs = []
+        for i, d in enumerate(dsts):
+            rid, pid = topo.addr(d, core)
+            es = topo.engines(core, d)[ENG_OUT * i:ENG_OUT * i + ENG_OUT]
+            at = place_of(T, topo, owner, d)
+            if req:
+                s_ap, d_ap = T[src][:, i, :], T[dname][:, at, :]
+            else:
+                s_ap, d_ap = T[src][:, i:i + 1], T[dname][:, at:at + 1]
+            trs.append(RemoteDMATransfer(dst_ids=[DstId(rid=rid, pnc=pid)], dma_engine_mask=emask(es), remote_sem=T.sem[sem_out],
+                                         src=s_ap, dst=d_ap))
+            n += len(es)
+        g.remote_dma_fused(trs, local_sem=T.sem.loc)
+    g.wait_ge(T.sem.loc, n)
+
+
+def plan(tasks):
+    n = len(tasks)
+    fin, free, order, ready = {}, {}, {}, {}
+    pre = [t["deps"] | t["odeps"] | ({t["aft"][0]} if t["aft"] else set()) for t in tasks]
+    pend = [len(x) for x in pre]
+    succ = [[] for _ in tasks]
+    for i, x in enumerate(pre):
+        for d in x:
+            succ[d].append(i)
+    tail = [0.0] * n
+    for i in range(n - 1, -1, -1):
+        tail[i] = tasks[i]["cost"] + WAKE + max([0.0] + [tail[x] for x in succ[i] if tasks[x]["prio"] <= tasks[i]["prio"]])
+
+    def enter(i):
+        t = tasks[i]
+        e = max([0.0] + [fin[d] + WAKE for d in t["deps"]] + [fin[d] for d in t["odeps"]])
+        if t["aft"]:
+            e = max(e, fin[t["aft"][0]] + t["aft"][1])
+        ready.setdefault(t["q"], {})[i] = e
+    for i in range(n):
+        if pend[i] == 0:
+            enter(i)
+    while len(fin) < n:
+        m, q = min((max(free.get(q, 0.0), min(l.values())), q) for q, l in ready.items() if l)
+        l, fr = ready[q], free.get(q, 0.0)
+        st = {i: max(fr, e) for i, e in l.items()}
+        pick = min(l, key=lambda i: (tasks[i]["prio"], max(st[i] - m - SLACK, 0.0), -tail[i], i))
+        if st[pick] > m + SLACK:
+            fits = [i for i in l if st[i] + tasks[i]["cost"] <= st[pick] + SLACK2]
+            now = [i for i in fits if st[i] <= m + SLACK]
+            if now:
+                pick = min(now, key=lambda i: (tasks[i]["prio"], -tail[i], i))
+            elif fits:
+                pick = min(fits, key=lambda i: (st[i], tasks[i]["prio"], i))
+        fin[pick] = st[pick] + tasks[pick]["cost"]
+        free[q] = fin[pick]
+        fin[pick] += tasks[pick]["lat"]
+        order.setdefault(q, []).append(pick)
+        del l[pick]
+        for x in succ[pick]:
+            pend[x] -= 1
+            if pend[x] == 0:
+                enter(x)
+    return order
+
+
+def runs(v):
+    out, i = [], 0
+    while i < len(v):
+        j, st = i + 1, (v[i + 1] - v[i] if i + 1 < len(v) else 0)
+        while j < len(v) and v[j] - v[j - 1] == st:
+            j += 1
+        out.append((i, j - i, v[i], st if j - i > 1 else 0))
+        i = j
+    return out
+
+
+def rank_program(g, core, T, topo):
+    rank = T.rank_of(core)
+    if rank is None:
+        for c in T.cores:
+            if c in topo.cores_of(core) and core in wiring(T, topo, c)[2]:
+                relay_program(g, core, T, topo, c)
+        return
+    cross, direct, rel = wiring(T, topo, core)
+    prank = [T.cores.index(c) for c in cross + direct]
+    base = NT * rank
+    SH = base - LO
+    tasks, wr, rd = [], {}, {}
+    V, S, E = g.vector, g.scalar, g.tensor
+    cy = 0.00083
+
+    def add(q, fn, reads, writes, cost, prio=1, ext=(), aft=None):
+        i = len(tasks)
+        deps, odeps = set(), set()
+        for b in reads:
+            if b in wr:
+                deps.add(wr[b])
+            if b in PSUM:
+                deps.update(x for x in rd.get(b, ()) if tasks[x]["q"] != q)
+        for b in writes:
+            if b in wr:
+                (odeps if q == "T" and tasks[wr[b]]["q"] == "T" else deps).add(wr[b])
+            deps.update(rd.get(b, ()))
+        tasks.append(dict(q=q, fn=fn, deps=deps, odeps=odeps, cost=cost, prio=prio, ext=tuple(ext), aft=aft, dma=None, lat=0.0))
+        for b in reads:
+            rd.setdefault(b, []).append(i)
+        for b in writes:
+            wr[b] = i
+            rd[b] = []
+        return i
+
+    def vop(fn, reads, writes, n, prio=1, ext=(), aft=None, f=1.0):
+        return add("V", lambda: [fn()], reads, writes, (0.02 if f == int(f) else 0.07) + 1.2 * cy * max(64, n * f), prio, ext, aft)
+
+    def ts(out, on, in0, inn, s1, s2, op0, op1=None, n=24, prio=1, ext=(), aft=None, extra=()):
+        if op1 is None:
+            return vop(lambda: V.tensor_scalar(out, in0, s1, None, op0), [inn] + list(extra), [on], n, prio, ext, aft)
+        return vop(lambda: V.tensor_scalar(out, in0, s1, s2, op0, op1), [inn] + list(extra), [on], n, prio, ext, aft)
+
+    def tt(out, on, in0, n0, in1, n1, op, n=24, prio=1, ext=(), aft=None, extra=(), f=1.0):
+        return vop(lambda: V.tensor_tensor(out, in0, in1, op), [n0, n1] + list(extra), [on], n, prio, ext, aft, f)
+
+    def cp(out, on, in_, inn, n=24, prio=1, extra=(), f=1.0):
+        return vop(lambda: V.tensor_copy(out, in_), [inn] + list(extra), [on], n, prio, f=f)
+
+    def fill(ap, on, v, n, prio=1):
+        return vop(lambda: V.memset(ap, v), [], [on], n, prio)
+
+    def act(out, on, in_, inn, n, prio=1, **kw):
+        return add("S", lambda: [S.activation(out, in_, F.Copy, **kw)], inn, [on], 0.03 + 1.2 * cy * max(64, n), prio)
+
+    def iota(ap, on, pat, b, ch, n, prio=1, fl=True):
+        if fl:
+            return add("G", lambda: [g.iota(ap, pat, b, ch, allow_small_or_imprecise_dtypes=True)], [], [on], 0.15 + 2.2 * cy * n, prio)
+        return add("G", lambda: [g.iota(ap, pat, b, ch)], [], [on], 0.15 + 2.2 * cy * n, prio)
+
+    def gfill(ap, on, v, n, prio=1):
+        return iota(ap, on, [[0, n]], v, 0, n, prio)
+
+    def mm(lst, reads, bank, prio=1):
+        c = sum((0.03 + 0.0008 * max(64, n) * (4 if f4 else 1)) for (_, n, f4) in lst)
+        return add("T", lambda: [E.matmul(*a) for (a, n, f4) in lst], reads, [bank], c, prio)
+
+    loads = {}
+
+    def load(q, sem, fn, cnt, deps, writes, cost, lat, prio=0):
+        i = add(q, fn, deps, writes, cost, prio)
+        tasks[i]["dma"] = sem
+        tasks[i]["lat"] = lat
+        loads[sem] = loads.get(sem, 0) + 16 * cnt
+        return i
+
+    def ld_pts(q, fs):
+        return [q.dma_start(T.X[4 * f + i:128:16, :], T.pts[i:24:3, :]) for f in fs for i in range(3)]
+    xset = fill(T.X[:], "X", 1, NP, 0)
+    load("Y", "ldA", lambda: [g.sync.dma_start(T.L0[:], T.tet0[:])], 1, [], ["L0"], 0.1, 2.0)
+    l1 = load("Y", "ldP", lambda: ld_pts(g.sync, (0, 1)), 6, [], ["Xa"], 0.6, 3.0)
+    load("S", "ldP", lambda: ld_pts(g.scalar, (2, 3)), 6, [], ["X"], 0.6, 3.0)
+    tasks[l1]["deps"].add(xset)
+    load("Y", "ldB", lambda: [g.sync.dma_start(T.PW[16 * k:16 * k + 16, LO:HI], T.planes[:]) for k in range(8)], 8, [], ["PW"], 0.8, 4.0)
+
+    iota(T.pi[:], "pi", [[0, 4]], 0, 1, 4, -5, False)
+    iota(T.md16[:], "md16", [[1, 8], [0, 16]], 0, 0, 128, -3)
+    iota(T.oRi[:], "oRi", [[0, 4], [-8, 3]], 24, 0, 12, -4)
+    iota(T.mk[:], "mk", [[1, 128]], 0, -1, 128, -3)
+    iota(T.jm[:], "jm", [[0, 24], [1, 16]], 0, 0, NP, -2)
+    CQ, CQB, CS = [], [], []
+    for s, n, a, st in runs(prank + [rank]):
+        iota(T.cQ[:, 24 * s:24 * (s + n)], "cQ%d" % s, [[st, n], [0, 24]], a, 0, 24 * n, -4)
+        CQ.append("cQ%d" % s)
+    iota(T.oKi[:], "oKi", [[1, 24]], 0, 0, 24, 0, False)
+    iota(T.cOw[:], "cOw", [[16, 24]], 128, 1, 24, 0)
+    iota(T.cD[:, 0:168], "cD", [[16, 7], [0, 24]], -1, 0, 168, 0)
+    iota(T.NB[:], "NB", [[1, PWID]], SH, 0, PWID, 1, False)
+    load("S", "ldC", lambda: [g.scalar.dma_start(T.NB[16 * k:16 * k + 16:4, LO:HI], T.nbr[:]) for k in range(8)], 8, [], ["NB"], 0.8, 3.5)
+    iota(T.K0[:], "K0", [[0, 24], [1, 5]], 0, 0, 120, 1)
+    iota(T.S1[:], "S1", [[4, 8], [1, 5]], -1, 0, 40, 1)
+    iota(T.S2[:], "S2", [[16, 8], [4, 5]], -4, -1, 40, 1)
+    iota(T.sC[:], "sC", [[16, 8], [0, 5]], 1, -1, 40, 1)
+    iota(T.Ms[:], "Ms", [[1, 8]], 0, 0, 8, 1)
+    iota(T.cD[:, 168:224], "cDB", [[16, 7], [0, 8]], -1, 0, 56, 4)
+    for s, n, a, st in runs(prank + [rank]):
+        iota(T.cQ[:, 192 + 8 * s:192 + 8 * (s + n)], "cQB%d" % s, [[st, n], [0, 8]], a, 0, 8 * n, 4)
+        CQB.append("cQB%d" % s)
+    for s, n, a, st in runs(prank):
+        iota(T.cS[:, s:s + n], "cS%d" % s, [[NT * st, n]], NT * a - SH, 0, n, 4)
+        CS.append("cS%d" % s)
+
+    ones = T.bc[0:1, 0:128]
+    fill(T.bc[:, 0:128], "one", 1.0, 64, 0)
+    fill(T.Rs[:, 0:168], "Rs", 1.0, 168, 0)
+    fill(T.Rs[:, 0:168:24], "Rs", 0.0, 7, 0)
+    fill(T.bc[:, 128:512], "c1k", 1024.0, 192, 0)
+    gfill(T.W1[:, 0:112], "W1", -1024, 112, 1)
+    gfill(T.PW[:, 0:LO], "PW0", 0, 8, 2)
+    gfill(T.PW[:, HI:PWID], "PW1", 0, 8, 2)
+    ts(T.pj[:, 0:1], "pj0", T.pi[:, 0:1], "pi", 15, None, A.bitwise_and, n=1, prio=0)
+    ts(T.pj[:, 1:2], "pj1", T.pi[:, 0:1], "pi", 4, None, A.arith_shift_right, n=1, prio=0)
+    ts(T.pj[:, 2:3], "pj2", T.pi[:, 0:1], "pi", 2, None, A.arith_shift_right, n=1, prio=0)
+    vop(lambda: V.tensor_copy(T.pf[:, 0:3], T.pj[:, 0:3]), ["pj0", "pj1", "pj2"], ["pf"], 3, 0)
+    p16, pg, p4 = T.pf[:, 0:1], T.pf[:, 1:2], T.pf[:, 2:3]
+    oK, oE, oR, oB8 = T.oT[:, 0:24], T.oT[:, 24:48], T.oT[:, 48:60], T.oT[:, 64:68]
+    ts(oR, "oR", T.oRi[:], "oRi", p16, None, A.add, n=12, prio=0, extra=["pf"])
+    ts(T.G16[:], "G16", T.md16[:], "md16", pg, None, A.is_equal, n=128, prio=0, extra=["pf"])
+    ts(T.I16[:], "I16", T.mk[:], "mk", 0.0, None, A.is_equal, n=128, prio=0)
+    cp(T.If[:], "If", T.I16[:], "I16", 128, 2)
+    ts(T.mk[:], "mk", T.mk[:], "mk", 0.0, -1.0, A.is_lt, A.mult, n=128, prio=0)
+    tt(T.U16[:], "U16", T.mk[:], "mk", T.G16[:], "G16", A.mult, n=128, prio=0, f=2)
+    cp(T.cO16[:], "cO16", T.cOw[:], "cOw", 24, 0)
+    cp(oK, "oK", T.oKi[:], "oKi", 24, 0)
+    ts(T.m16[:], "m16", T.jm[:], "jm", p16, None, A.is_equal, n=NP, prio=0, extra=["pf"])
+    ts(T.G2k[:], "G2k", T.md16[:], "md16", pg, 2048.0, A.is_equal, A.mult, n=128, prio=0, extra=["pf"])
+    ts(T.Rd[:], "Rd", T.jm[:], "jm", 1.0, None, A.is_ge, n=NP, prio=0)
+
+    def slots(oh, ohn, M, co, cqn, rkw, rkn, offs, offn, cdn, ro, rsn, su, sun, prio, cnt=None):
+        n7, n8 = 7 * M, 8 * M
+        cq, cd, rs = T.cQ[:, co:co + n8], T.cD[0:1, ro:ro + n7], T.Rs[:, ro:ro + n7]
+        sc, z1, z2 = T.scn, T.z1, T.z2
+        mm([((T.rB[:, n7:n8], T.I16[:], T.cO16[:, 0:M], True, True), M, 0),
+            ((T.rB[:, 0:n7], ones, cd, True, False), n7, 0)], ["I16", "cO16", "one", cdn], "rB", prio)
+        vop(lambda: V.tensor_tensor(oh[:, 0:n8], rkw.indirect(offs), cq, A.is_equal), rkn + offn + cqn, [ohn], n8, prio, f=1.5)
+        l = [((T.rA[:, 0:n7], T.G16[:], oh[:, 0:n7], True, cnt is None), n7, 0)]
+        if cnt is not None:
+            l.append(((T.rA[:, 0:n7:M], T.I16[:], cnt, False, True), 7, 0))
+        mm(l, ["G16", ohn] + (["I16", "cnt"] if cnt is not None else []), "rA", prio)
+        mm([((T.rB[:, 0:n7], T.U16[:], oh[:, 0:n7], False, True), n7, 0)], ["U16", ohn], "rB", prio)
+        vop(lambda: V.tensor_tensor_scan(sc[:, 0:n7], rs, T.rA[:, 0:n7], 0.0, A.mult, A.add), [rsn, "rA"], ["scn"], n7, prio)
+        vop(lambda: V.tensor_tensor(z2[:, 0:n8], T.rB[:, 0:n8], oh[:, 0:n8], A.mult), ["rB", ohn], ["z2"], n8, prio)
+        vop(lambda: V.tensor_tensor(z1[:, 0:n7], sc[:, 0:n7], oh[:, 0:n7], A.mult), ["scn", ohn], ["z1"], n7, prio, f=2)
+        mm([((T.rA[:, 0:M], T.I16[:], z2[:, M * b:M * b + M], b == 0, False), M, 0) for b in range(8)], ["I16", "z2"], "rA", prio)
+        mm([((T.rA[:, 0:M], T.I16[:], z1[:, M * b:M * b + M], False, b == 6), M, 0) for b in range(7)], ["I16", "z1"], "rA", prio)
+        cp(su[:, 0:M], sun, T.rA[:, 0:M], "rA", M, prio)
+
+    def pack(xap, xn, tib, k, prio, off1k):
+        n = 16 * k
+        if off1k:
+            mm([((T.rC[:, 0:n], ones, T.bc[0:1, 128:128 + n], True, False), n, 0)], ["one", "c1k"], "rC", prio)
+        vop(lambda: V.tensor_tensor(T.ex[:, 0:n], tib.indirect(T.oT[:, 0:k]), T.m16[:, 0:n], A.mult), ["ti", "oK", "m16"], ["ex"], n, prio, f=1.6)
+        mm([((T.rC[:, 0:n], T.G2k[:], T.ex[:, 0:n], not off1k, True), n, 0)], ["G2k", "ex"], "rC", prio)
+        tt(T.PK[:, 0:n], "PK", T.rC[:, 0:n], "rC", xap, xn, A.add, n=n, prio=prio)
+
+    def decode(W, wn, yi, yin, tl, tln, msg, msgn, prio):
+        tt(T.dg[:], "dg", W[:, 0:112], wn, T.m16[:, 0:112], "m16", A.mult, n=112, prio=prio, f=2)
+        ts(yi[:], yin, W[:, 0:112], wn, 2047, None, A.bitwise_and, n=112, prio=prio)
+        vop(lambda: V.tensor_tensor_scan(T.sd[:], T.Rd[:, 0:112], T.dg[:], 0.0, A.mult, A.add), ["Rd", "dg"], ["sd"], 112, prio)
+        ts(msg[:, :, 0:16], msgn, yi[:], yin, -1024.0, None, A.add, n=112, prio=prio)
+        ts(tl[:, 0:7], tln, T.sd[:, 15:112:16], "sd", 11, None, A.arith_shift_right, n=7, prio=prio)
+        cp(msg[:, :, 16], msgn, tl[:, 0:7], tln, 7, prio)
+
+    nloc = [0]
+
+    def send(src, srcn, hname, dname, sem, req, prio):
+        def fn():
+            own8 = topo.engines(core, direct[0])
+            alle = topo.engines(core, rel[0])
+            hop = [e for e in alle if e not in own8]
+            if len(hop) < ENG_HOP * N_REL:
+                hop = hop + [e for e in alle if e in own8]
+            trs = []
+            for k, r in enumerate(rel):
+                rid, pid = topo.addr(r, core)
+                s_ap = src[:, PER * k:PER * k + PER, :] if req else src[:, PER * k:PER * k + PER]
+                es = hop[ENG_HOP * k:ENG_HOP * k + ENG_HOP]
+                trs.append(RemoteDMATransfer(dst_ids=[DstId(rid=rid, pnc=pid)], dma_engine_mask=emask(es), remote_sem=T.sem[hname],
+                                             src=s_ap, dst=T[hname][:]))
+                nloc[0] += len(es)
+            g.remote_dma_fused(trs, local_sem=T.sem.loc)
+            trs = []
+            for k, d in enumerate(direct):
+                rid, pid = topo.addr(d, core)
+                es = topo.engines(core, d)[ENG_DIR * k:ENG_DIR * k + ENG_DIR]
+                b, at = len(cross) + k, place_of(T, topo, core, d)
+                if req:
+                    s_ap, d_ap = src[:, b, :], T[dname][:, at, :]
+                else:
+                    s_ap, d_ap = src[:, b:b + 1], T[dname][:, at:at + 1]
+                trs.append(RemoteDMATransfer(dst_ids=[DstId(rid=rid, pnc=pid)], dma_engine_mask=emask(es), remote_sem=T.sem[sem],
+                                             src=s_ap, dst=d_ap))
+                nloc[0] += len(es)
+            g.remote_dma_fused(trs, local_sem=T.sem.loc)
+            return []
+        return add("G", fn, [srcn], [], 1.0, prio)
+    ARR = ENG_OUT * len(cross) + ENG_DIR * len(direct)
+
+    def step(t, k, X, xn, w, wn, L, Ln, bK, bP, bL, prio, last=None, Lacc=None, Laccn=None):
+        B = 3 if k == 24 else 1
+        m, kc = 40 * B, 8 * B
+        pr, pa, u, c, kp, p, re, e = [T[x + t] for x in ("pr", "pa", "u", "c", "k", "p", "re", "e")]
+        nm = lambda x: x + t
+        part = lambda x, q: x + t + ("" if B == 1 else "_%d" % q)
+        lo = 256 if bK == bL else 0
+        for q, (a, z) in enumerate(((0, 16), (16, 24)) if B == 3 else ((0, k),)):
+            vop(lambda a=a, z=z: V.tensor_tensor(pr[:, 16 * a:16 * z], T.PW[:].indirect(w[:, a:z]), X[:, 16 * a:16 * z], A.mult),
+                ["PW", "PW0", "PW1", wn, xn], [part("pr", q)], 16 * (z - a), prio, f=1.6)
+            add("S", lambda a=a, z=z: [S.activation(pa[:, 16 * a:16 * z], T.ND[:].indirect(w[:, a:z]), F.Copy)], ["ND", wn], [part("pa", q)],
+                0.1 + 1.8 * cy * 16 * (z - a), prio)
+        for b in range(B):
+            mm([((T[bK][:, 40 * b:40 * b + 40], pr[:, 128 * b:128 * b + 128], T.S1[:], True, True), 40, 1)], [part("pr", b // 2), "S1"], bK, prio)
+        for b in range(B):
+            mm([((T[bP][:, 40 * b:40 * b + 40], pa[:, 128 * b:128 * b + 128], T.S2[:], True, True), 40, 1)], [part("pa", b // 2), "S2"], bP, prio)
+        Li, Lin = (L, Ln) if Lacc is None else (Lacc, Laccn)
+        il = lambda: mm([((T[bL][:, lo:lo + kc], T.If[:], Li[:, 0:kc], True, False), kc, 1)], ["If", Lin], bL, prio)
+        if bL != bK:
+            il()
+        vop(lambda: V.tensor_tensor_scan(u[:, 1:m + 1], T.R1c[:, 0:m], T[bK][:, 0:m], 0.0, A.max, A.min), ["R1c", bK], [nm("u")], m, prio)
+        vop(lambda: V.tensor_tensor(c[:, 0:m], T[bK][:, 0:m], u[:, 0:m], A.is_lt), [bK, nm("u"), nm("u0")], [nm("c")], m, prio)
+        if bL == bK:
+            il()
+        vop(lambda: V.tensor_tensor(kp[:, 0:m], T.K0[:, 0:m], c[:, 0:m], A.is_gt), ["K0", nm("c")], [nm("k")], m, prio, f=2)
+        vop(lambda: V.tensor_tensor(p[:, 0:m], T[bP][:, 0:m], c[:, 0:m], A.mult), [bP, nm("c")], [nm("p")], m, prio)
+        vop(lambda: V.tensor_tensor_scan(re[:, 0:m], kp[:, 0:m], p[:, 0:m], 0.0, A.mult, A.add), [nm("k"), nm("p")], [nm("re")], m, prio)
+        for q, (a, z) in enumerate(((0, 16), (16, 24)) if B == 3 else ((0, 8),)):
+            vop(lambda a=a, z=z: V.tensor_tensor(e[:, 16 * a:16 * z], re[:, 0:m].indirect(T.oT[:, 24 + a:24 + z]), T.m16[:, 16 * a:16 * z], A.mult),
+                [nm("re"), "oE", "m16"], [part("e", q)], 16 * (z - a), prio, f=1.6)
+        for b in range(B):
+            mm([((T[bL][:, lo + 8 * b:lo + 8 * b + 8], e[:, 128 * b:128 * b + 128], T.Ms[:], False, b == B - 1), 8, 1)],
+               [part("e", b // 2), "Ms"], bL, prio)
+        if last is not None:
+            cp(last[0][:, 0:k], last[1], T[bL][:, lo:lo + k], bL, k, prio)
+        else:
+            ts(w[:, 0:k], wn, T[bL][:, lo:lo + k], bL, 0.0, float(HI), A.max, A.min, n=k, prio=prio)
+            act(L[:, 0:kc], Ln, T[bL][:, lo:lo + kc], [bL], kc, prio)
+
+    ts(T.rk[:, 24:40], "rka", T.L0[:, 0:16], "L0", 10, None, A.arith_shift_right, prio=0)
+    ts(T.rk[:, 8:24], "rkb", T.L0[:, 8:24], "L0", 10, None, A.arith_shift_right, prio=0)
+    gfill(T.rk[:, 0:8], "rkz", -1, 8, 0)
+    gfill(T.rk[:, 40:48], "rkz2", -1, 8, 0)
+    RK = ["rka", "rkb", "rkz", "rkz2"]
+    ts(T.ti[:], "ti", T.L0[:], "L0", 1023, None, A.bitwise_and, prio=0)
+    slots(T.oh1, "oh1", 24, 0, CQ, T.rk[:], RK, oR, ["oR"], "cD", 0, "Rs", T.su1, "su1", 0)
+    pack(T.X[:], "X", T.ti[:], 24, 0, True)
+    cp(T.W1[:].indirect(T.su1[:]), "W1", T.PK[:], "PK", NP, 0, extra=["su1"], f=3.5)
+    decode(T.W1, "W1", T.yi1, "yi1", T.tl1, "tl1", T.msg1, "msg1", 0)
+    s1 = send(T.msg1, "msg1", "hq1", "land1", "rq1", True, 0)
+
+    ts(T.K0[:], "K0", T.K0[:], "K0", 1.0, None, A.is_ge, n=120, prio=2)
+    act(T.R1c[:], "R1c", T.K0[:], ["K0"], 120, 2, scale=-BIG)
+    ts(T.S1[:], "S1", T.S1[:], "S1", p4, None, A.is_equal, n=40, prio=2, extra=["pf"])
+    tt(T.S1[:], "S1", T.S1[:], "S1", T.K0[:, 0:40], "K0", A.mult, n=40, prio=2)
+    ts(T.S2[:], "S2", T.S2[:], "S2", 0.0, None, A.is_equal, n=40, prio=2)
+    ts(T.sC[:], "sC", T.sC[:], "sC", 0.0, None, A.is_equal, n=40, prio=2)
+    tt(T.S2[:], "S2", T.S2[:], "S2", T.sC[:], "sC", A.subtract, n=40, prio=2)
+    tt(T.S2[:], "S2", T.S2[:], "S2", T.K0[:, 0:40], "K0", A.mult, n=40, prio=2)
+    ts(T.Ms[:], "Ms", T.Ms[:], "Ms", pg, None, A.is_equal, n=8, prio=2, extra=["pf"])
+    ts(oE, "oE", T.oKi[:], "oKi", 5.0, 4.0, A.mult, A.add, n=24, prio=2)
+    for t in ("O", "V", "R"):
+        gfill(T["u" + t][:, 0:1], "u0" + t, 0, 1, 2)
+    for t in ("V", "R"):
+        gfill(T["pr" + t][:, 112:128], "pr" + t, 0, 16, 2)
+        gfill(T["pa" + t][:, 112:128], "pa" + t, 0, 16, 2)
+    gfill(T.Lv[:, 7:8], "Lv", 0, 1, 2)
+    gfill(T.Lv0[:, 7:8], "Lv0", 0, 1, 2)
+    cp(T.ND[:], "ND", T.NB[:], "NB", PWID, 3)
+    ts(T.Lo[:], "Lo", T.L0[:], "L0", float(-SH) - DEAD, None, A.add, prio=2)
+    tt(T.Lo[:], "Lo", T.Lo[:], "Lo", T.oh1[:, 168:192], "oh1", A.mult, prio=2)
+    ts(T.Lo[:], "Lo", T.Lo[:], "Lo", DEAD, None, A.add, prio=2)
+    ts(T.wO[:], "wO", T.Lo[:], "Lo", 0.0, float(HI), A.max, A.min, prio=2)
+    own = lambda pr: step("O", 24, T.X, "X", T.wO, "wO", T.Lo, "Lo", "oK", "oP", "oK", pr)
+    own(P_O1)
+
+    def visitors(land, ln, out, outn, sem, sent):
+        add("V", lambda: [V.tensor_scalar(T.wv[:, 0:7], land[:, :, 16], 8.0, None, A.add)], [], ["wv", ln], 0.08, 0, [(sem, ARR)], (sent, FLY_REQ))
+        cp(T.Xv[:], "Xv", land[:, :, 0:16], ln, 112, 0)
+        add("V", lambda: [V.tensor_scalar(T.Lv0[:, 0:7], land[:, :, 16], 8.0, None, A.add)], [ln], ["Lv0"], 0.08, 1)
+        act(T.Lv[:, 0:7], "Lv", T.Lv0[:, 0:7], ["Lv0"], 7, 1)
+        a = (7, T.Xv, "Xv", T.wv, "wv", T.Lv, "Lv", "vK", "vP", "vL", 0)
+        step("V", *a)
+        step("V", *a)
+        tt(T.Ld[:], "Ld", T.Lv[:], "Lv", T.Lv0[:], "Lv0", A.subtract, n=8, prio=0)
+        step("V", *a, last=(out, outn), Lacc=T.Ld, Laccn="Ld")
+
+    visitors(T.land1, "land1", T.out1, "out1", "rq1", s1)
+    s2 = send(T.out1, "out1", "hp1", "rep1", "rp1", False, 0)
+
+    ts(T.sBv[:, 0:7], "sBv", T.tl1[:, 0:7], "tl1", -DEAD, None, A.add, n=7, prio=4)
+    tt(T.sBv[:, 0:7], "sBv", T.sBv[:, 0:7], "sBv", T.cS[:, 0:7], CS[0], A.add, n=7, prio=4, extra=CS[1:])
+    ts(T.sBg[:, 0:7], "sBg", T.tl1[:, 0:7], "tl1", 0.0, None, A.is_ge, n=7, prio=4)
+    tt(T.sBv[:, 0:7], "sBv", T.sBv[:, 0:7], "sBv", T.sBg[:, 0:7], "sBg", A.mult, n=7, prio=4)
+    ts(T.sBv[:, 0:7], "sBv", T.sBv[:, 0:7], "sBv", DEAD, None, A.add, n=7, prio=4)
+    ts(T.xB[:], "xB", T.yi1[:], "yi1", -1024.0, None, A.add, n=112, prio=5)
+    gfill(T.W2[:, 0:112], "W2", -1024, 112, 3)
+    gfill(T.Rs[:, 168:224], "RsB", 1, 56, 4)
+    gfill(T.Rs[:, 168:224:8], "RsB", 0, 7, 4)
+    gfill(T.rkB[:, 7:8], "rkB", rank, 1, 4)
+    fill(T.Lb[:, 7:8], "Lb", DEAD, 1, 4)
+    ts(T.pj[:, 4:8], "pj4", T.pi[:], "pi", 7, None, A.bitwise_and, n=4, prio=4)
+    cp(oB8, "oB8", T.pj[:, 4:8], "pj4", 4, 4)
+    own(P_O2)
+    own(P_O2)
+
+    RKC = (SH - 511.1875) / 1024.0
+    ts(T.rk[:, 24:40], "rka", T.Lo[:, 0:16], "Lo", 1.0 / 1024, RKC, A.mult, A.add, prio=P_A)
+    ts(T.rk[:, 8:24], "rkb", T.Lo[:, 8:24], "Lo", 1.0 / 1024, RKC, A.mult, A.add, prio=P_A)
+    ts(T.ci[:], "ci", T.Lo[:], "Lo", float(SH), None, A.add, prio=P_A)
+    ts(T.ti[:], "ti", T.ci[:], "ci", 1023, None, A.bitwise_and, prio=P_A)
+    slots(T.ohA, "ohA", 24, 0, CQ, T.rk[:], RK, oR, ["oR"], "cD", 0, "Rs", T.suA, "suA", P_A)
+    cp(T.cnt[:, 0:7], "cnt", T.scn[:, 23:168:24], "scn", 7, P_A)
+    pack(T.X[:], "X", T.ti[:], 24, P_A, True)
+    cp(T.W2[:].indirect(T.suA[:]), "W2", T.PK[:], "PK", NP, P_A, extra=["suA"], f=3.5)
+
+    vop(lambda: V.tensor_tensor(T.Lb[:, 0:7], T.sBv[:, 0:7], T.rep1[:, 0:7], A.add), ["sBv"], ["Lb"], 7, 0, [("rp1", ARR)], (s2, FLY_REP))
+    ts(T.rkB[:, 0:7], "rkB", T.Lb[:, 0:7], "Lb", 1.0 / 1024, RKC, A.mult, A.add, n=7, prio=0)
+    ts(T.ci[:, 0:7], "ci", T.Lb[:, 0:7], "Lb", float(SH), None, A.add, n=7, prio=0)
+    ts(T.ti[:, 0:7], "ti", T.ci[:, 0:7], "ci", 1023, None, A.bitwise_and, n=7, prio=0)
+    slots(T.ohA, "ohA", 8, 192, CQB, T.rkB[:], ["rkB"], oB8, ["oB8"], "cDB", 168, "RsB", T.suB, "suB", 0, cnt=T.cnt[:, 0:7])
+    pack(T.yi1[:], "yi1", T.ti[:, 0:8], 7, 0, False)
+    cp(T.W2[:].indirect(T.suB[:, 0:7]), "W2", T.PK[:, 0:112], "PK", 112, 0, extra=["suB"], f=3.5)
+    decode(T.W2, "W2", T.yi2, "yi2", T.tl2, "tl2", T.msg2, "msg2", 0)
+    s3 = send(T.msg2, "msg2", "hq2", "land2", "rq2", True, 0)
+
+    ts(T.wr[:, 0:7], "wr", T.Lb[:, 0:7], "Lb", 0.0, float(HI), A.max, A.min, n=7, prio=P_C)
+    cp(T.Gf[:], "Gf", T.G16[:], "G16", 128, P_C)
+    gfill(T.vW[:, 112:120], "vW", 0, 8, 4)
+    gfill(T.dW[:, 112:136], "dW", 0, 24, 4)
+    for _ in range(3):
+        step("R", 7, T.xB, "xB", T.wr, "wr", T.Lb, "Lb", "rA", "rB", "rC", P_R)
+        own(P_O3)
+    visitors(T.land2, "land2", T.out2, "out2", "rq2", s3)
+    s4 = send(T.out2, "out2", "hp2", "rep2", "rp2", False, 0)
+
+    ts(T.s1c[:], "s1c", T.su1[:], "su1", 112.0, None, A.min, prio=P_C)
+    ts(T.smA[:], "smA", T.suA[:], "suA", 128.0, None, A.min, prio=P_C)
+    ts(T.smB[:, 0:7], "smB", T.suB[:, 0:7], "suB", 128.0, None, A.min, n=7, prio=P_C)
+    ts(T.vB[:, 0:7], "vB", T.Lb[:, 0:7], "Lb", 8192.0, 256.0, A.add, A.mult, n=7, prio=P_C)
+    tt(T.vB[:, 0:7], "vB", T.vB[:, 0:7], "vB", T.smB[:, 0:7], "smB", A.add, n=7, prio=P_C)
+    vop(lambda: V.tensor_tensor(T.exv[:], T.vB[:, 0:7].indirect(T.oT[:, 0:7]), T.m16[:, 0:112], A.mult), ["vB", "oK", "m16"], ["exv"], 112, P_C, f=1.6)
+    mm([((T.rC[:, 0:112], T.Gf[:], T.exv[:], True, True), 112, 1)], ["Gf", "exv"], "rC", P_C)
+    cp(T.vW[:, 0:112], "vW", T.rC[:, 0:112], "rC", 112, P_C)
+    vop(lambda: V.tensor_tensor(T.gv[:], T.vW[:].indirect(T.s1c[:]), T.m16[:], A.mult), ["vW", "s1c", "m16"], ["gv"], NP, P_C, f=1.6)
+    vop(lambda: V.tensor_tensor_scan(T.sv[:], T.Rd[:], T.gv[:], 0.0, A.mult, A.add), ["Rd", "gv"], ["sv"], NP, P_C)
+    ts(T.vO[:], "vO", T.Lo[:], "Lo", 8192.0, 256.0, A.add, A.mult, prio=P_C)
+    tt(T.vO[:], "vO", T.vO[:], "vO", T.smA[:], "smA", A.add, prio=P_C)
+    tt(T.vO[:], "vO", T.vO[:], "vO", T.oh1[:, 168:192], "oh1", A.mult, prio=P_C)
+    tt(T.vt[:], "vt", T.vO[:], "vO", T.sv[:, 15:NP:16], "sv", A.add, prio=P_C)
+    ts(T.ci[:], "ci", T.vt[:], "vt", 255, None, A.bitwise_and, prio=P_C)
+    cp(T.tau[:], "tau", T.ci[:], "ci", 24, P_C)
+    ts(T.vt[:], "vt", T.vt[:], "vt", 8, None, A.arith_shift_right, prio=P_C)
+    ts(T.Yb[:], "Yb", T.vt[:], "vt", float(SH - 8192), None, A.add, prio=P_C)
+
+    vop(lambda: V.tensor_tensor(T.exv[:], T.rep2[:, 0:7].indirect(T.oT[:, 0:7]), T.m16[:, 0:112], A.mult), ["oK", "m16"], ["exv"], 112, 0,
+        [("rp2", ARR)], (s4, FLY_REP), f=1.6)
+    mm([((T.rC[:, 0:112], T.Gf[:], T.exv[:], True, True), 112, 1)], ["Gf", "exv"], "rC", 0)
+    cp(T.dW[:, 0:112], "dW", T.rC[:, 0:112], "rC", 112, 0)
+    vop(lambda: V.tensor_tensor(T.gv[:], T.dW[:].indirect(T.tau[:]), T.m16[:], A.mult), ["dW", "tau", "m16"], ["gv"], NP, 0, f=1.6)
+    vop(lambda: V.tensor_tensor_scan(T.sv[:], T.Rd[:], T.gv[:], 0.0, A.mult, A.add), ["Rd", "gv"], ["sv"], NP, 0)
+    tt(T.vO[:], "vO", T.sv[:, 15:NP:16], "sv", T.Yb[:], "Yb", A.add, prio=0)
+    load("Y", "st", lambda: [g.sync.dma_start(T.y[:], T.vO[:])], 1, ["vO"], [], 0.1, 0.0)
+
+    order = plan(tasks)
+    queue = {"V": V, "S": S, "T": E, "G": g, "Y": g.sync}
+    semof = {"V": "sV", "S": "sS", "T": "sT", "G": "sG"}
+    done, know, total = {}, {}, {}
+    ptr = {q: 0 for q in order}
+    known = {q: {} for q in order}
+    left = len(tasks)
+    while left:
+        before = left
+        for q in order:
+            while ptr[q] < len(order[q]):
+                i = order[q][ptr[q]]
+                t = tasks[i]
+                if any(d not in done for d in t["deps"]):
+                    break
+                kq = known[q]
+                for d in sorted(t["deps"], key=lambda d: (-len(know[d]), -done[d][1])):
+                    s, v = done[d]
+                    if s is None or kq.get(s, 0) >= v:
+                        continue
+                    v = max(done[x][1] for x in t["deps"] if done[x][0] == s)
+                    if any(done[x][0] not in (s, None) and know[x].get(s, 0) >= v and kq.get(done[x][0], 0) < done[x][1] for x in t["deps"]):
+                        continue
+                    queue[q].wait_ge(T.sem[s], v)
+                    for x in t["deps"]:
+                        if done[x][0] == s:
+                            for s2, v2 in know[x].items():
+                                kq[s2] = max(kq.get(s2, 0), v2)
+                    kq[s] = max(kq.get(s, 0), v)
+                for s, v in t["ext"]:
+                    if kq.get(s, 0) < v:
+                        queue[q].wait_ge(T.sem[s], v)
+                        kq[s] = v
+                ins = t["fn"]()
+                if t["dma"]:
+                    for x in ins:
+                        x.then_inc(T.sem[t["dma"]], 16)
+                    done[i] = (t["dma"], loads[t["dma"]])
+                elif not ins:
+                    done[i] = (None, 0)
+                else:
+                    s = semof[q]
+                    for x in ins:
+                        x.then_inc(T.sem[s], 1)
+                    total[s] = total.get(s, 0) + len(ins)
+                    done[i] = (s, total[s])
+                know[i] = dict(kq)
+                if done[i][0] is not None:
+                    know[i][done[i][0]] = done[i][1]
+                ptr[q] += 1
+                left -= 1
+        if left == before:
+            raise ValueError("the order can't be emitted")
+    for s, v in sorted(total.items()):
+        g.wait_ge(T.sem[s], v)
+    for s, v in loads.items():
+        g.wait_ge(T.sem[s], v)
+    for s in ("rq1", "rp1", "rq2", "rp2"):
+        g.wait_ge(T.sem[s], ARR)
+    g.wait_ge(T.sem.loc, nloc[0])

@@ -6,29 +6,30 @@ LO, HI, PWID = 8, 1032, 1040
 DEAD = 7.375
 MSG = 17
 WIN = 640
-BIG = 8388608.0
+BIG, MID = 8388608, 4194304
+NONE = (1 << 21) + 1024
 N_REL, ENG_HOP, ENG_OUT, ENG_DIR = 2, 4, 4, 2
 PER = 4 // N_REL
 
 _sb = {
     "X": ([128, NP], "int32"), "L0": ([128, NK], "int32"), "PW": ([128, PWID], "int32"), "NB": ([128, PWID], "int32"),
     "ND": ([128, PWID], "float32"), "Xv": ([128, 112], "float32"), "xB": ([128, 112], "float32"),
-    "pi": ([128, 4], "int32"), "pj": ([128, 8], "int32"), "pf": ([128, 4], "float32"), "jm": ([128, NP], "float32"),
-    "mk": ([128, 128], "float32"), "md16": ([128, 128], "float32"), "m16": ([128, NP], "float32"), "Rd": ([128, NP], "float32"),
+    "pi": ([128, 4], "int32"), "pj": ([128, 8], "int32"), "pf": ([128, 8], "float32"), "jm": ([128, 128], "bfloat16"), "x1": ([128, NK], "int32"),
+    "mk": ([128, 128], "float32"), "md16": ([128, 128], "float32"), "m16": ([128, NP], "bfloat16"), "Rd": ([128, NP], "float32"),
     "G16": ([128, 128], "float16"), "G2k": ([128, 128], "float16"), "Gf": ([128, 128], "float32"),
     "U16": ([128, 128], "float16"), "I16": ([128, 128], "float16"), "If": ([128, 128], "float32"),
-    "S1": ([128, 40], "float32"), "S2": ([128, 40], "float32"), "sC": ([128, 40], "float32"), "Ms": ([128, 8], "float32"),
-    "K0": ([128, 120], "float32"), "R1c": ([128, 120], "float32"),
+    "S1": ([128, 48], "float32"), "S2": ([128, 48], "float32"), "sA": ([128, 48], "float32"), "sC": ([128, 49], "float32"), "Ms": ([128, 8], "float32"),
+    "R1c": ([128, 144], "float32"), "scC": ([128, 192], "float32"), "scD": ([128, 112], "float32"), "I1k": ([128, 128], "float16"),
     "oKi": ([128, NK], "int32"), "oRi": ([128, 12], "float32"), "oT": ([128, 72], "uint16"),
-    "Rs": ([128, 224], "float32"), "cQ": ([128, 256], "float32"), "cD": ([128, 224], "bfloat16"), "bc": ([128, 512], "bfloat16"),
+    "Rs": ([128, 224], "float32"), "cQ": ([128, 256], "float32"), "cD": ([128, 8], "bfloat16"), "bc": ([128, 128], "bfloat16"),
     "cOw": ([128, NK], "float32"), "cO16": ([128, NK], "float16"), "cS": ([128, 8], "float32"),
-    "rk": ([128, 48], "int32"), "ci": ([128, NK], "int32"), "ti": ([128, NK], "int32"), "rkB": ([128, 8], "int32"),
-    "oh1": ([128, 192], "float16"), "ohA": ([128, 192], "float16"), "ex": ([128, NP], "float16"), "scn": ([128, 168], "float32"),
+    "rk": ([128, 32], "int32"), "ci": ([128, NK], "int32"), "ti": ([128, NK], "int32"), "tf": ([128, NK], "float32"), "rkB": ([128, 8], "int32"),
+    "oh1": ([128, 192], "float16"), "ohA": ([128, 192], "float16"), "ex": ([128, NP], "float16"),
+    "scn": ([128, 64], "float32"), "zz": ([128, 64], "float32"), "mx": ([128, 56], "float32"),
     "z1": ([128, 168], "float16"), "z2": ([128, 192], "float16"), "cnt": ([128, 8], "float16"), "PK": ([128, NP], "int32"),
     "su1": ([128, NK], "uint16"), "suA": ([128, NK], "uint16"), "suB": ([128, 8], "uint16"),
     "W1": ([128, WIN], "int32"), "W2": ([128, WIN], "int32"),
-    "dg": ([128, 112], "float32"), "sd": ([128, 112], "int32"), "yi1": ([128, 112], "int32"), "yi2": ([128, 112], "int32"),
-    "tl1": ([128, 8], "int32"), "tl2": ([128, 8], "int32"),
+    "sd": ([128, 112], "int32"), "yi1": ([128, 7, MSG], "int32"), "yi2": ([128, 7, MSG], "int32"), "yB": ([128, 112], "int32"),
     "msg1": ([128, 7, MSG], "float16"), "msg2": ([128, 7, MSG], "float16"),
     "land1": ([128, 7, MSG], "float16"), "land2": ([128, 7, MSG], "float16"),
     "sBv": ([128, 8], "float32"), "sBg": ([128, 8], "float32"),
@@ -42,8 +43,8 @@ _sb = {
     "hq1": ([128, PER, MSG], "float16"), "hq2": ([128, PER, MSG], "float16"), "hp1": ([128, PER], "float32"), "hp2": ([128, PER], "float32"),
 }
 for _t, _n in (("O", 384), ("V", 128), ("R", 128)):
-    _m = _n // 128 * 40
-    for _b, _w in (("pr", _n), ("pa", _n), ("u", _m + 8), ("c", _m), ("k", _m), ("p", _m), ("re", _m), ("e", _n)):
+    _m = _n // 128 * 48
+    for _b, _w in (("pr", _n), ("pa", _n), ("u", _m + 8), ("k", _m), ("re", _m), ("e", _n)):
         _sb[_b + _t] = ([128, _w], "float32")
 SCRATCH = {_k: ("sbuf", _v[0], _v[1]) for _k, _v in _sb.items()}
 PSUM = ("oK", "oP", "vK", "vP", "vL", "rA", "rB", "rC")
@@ -51,9 +52,9 @@ for _k in PSUM:
     SCRATCH[_k] = ("psum", [128, 512], "float32")
 SEMAPHORES = ["sV", "sS", "sT", "sG", "ldA", "ldP", "ldB", "ldC", "st", "rq1", "rq2", "rp1", "rp2", "hq1", "hq2", "hp1", "hp2", "loc"]
 
-FLY_REQ, FLY_REP = 6.5, 6.5
-WAKE, SLACK, SLACK2 = 0.06, 0.1, 0.2
-P_O1, P_O2, P_A, P_O3, P_R, P_C = 3, 2, 2, 5, 4, 4
+FLY = (9, 6.5, 6, 5)
+WAKE, SLACK, SLACK2 = 0.1, 0.1, 0.1
+P_O1, P_O2, P_A, P_O3, P_R, P_C = 2, 2, 1, 5, 4, 4
 
 
 def wiring(T, topo, core):
@@ -233,33 +234,38 @@ def rank_program(g, core, T, topo):
 
     def ld_pts(q, fs):
         return [q.dma_start(T.X[4 * f + i:128:16, :], T.pts[i:24:3, :]) for f in fs for i in range(3)]
-    xset = fill(T.X[:], "X", 1, NP, 0)
-    load("Y", "ldA", lambda: [g.sync.dma_start(T.L0[:], T.tet0[:])], 1, [], ["L0"], 0.1, 2.0)
-    l1 = load("Y", "ldP", lambda: ld_pts(g.sync, (0, 1)), 6, [], ["Xa"], 0.6, 3.0)
-    load("S", "ldP", lambda: ld_pts(g.scalar, (2, 3)), 6, [], ["X"], 0.6, 3.0)
-    tasks[l1]["deps"].add(xset)
+
+    fill(T.bc[:, 0:128], "one", 1.0, 64, -10)
+    fill(T.x1[:], "x1", 1, NK, -9)
+    load("Y", "ldA", lambda: [g.sync.dma_start(T.L0[:], T.tet0[:])], 1, [], ["L0"], 0.1, 2.0, -9)
+    load("Y", "ldP", lambda: ld_pts(g.sync, (0, 1)) + [g.sync.dma_start(T.X[4 * f + 3:128:16, :], T.x1[:]) for f in range(4)],
+         10, ["x1"], ["Xa"], 1.0, 2.0)
+    load("S", "ldP", lambda: ld_pts(g.scalar, (2, 3)), 6, [], ["X"], 0.6, 2.5)
     load("Y", "ldB", lambda: [g.sync.dma_start(T.PW[16 * k:16 * k + 16, LO:HI], T.planes[:]) for k in range(8)], 8, [], ["PW"], 0.8, 4.0)
 
-    iota(T.pi[:], "pi", [[0, 4]], 0, 1, 4, -5, False)
-    iota(T.md16[:], "md16", [[1, 8], [0, 16]], 0, 0, 128, -3)
-    iota(T.oRi[:], "oRi", [[0, 4], [-8, 3]], 24, 0, 12, -4)
-    iota(T.mk[:], "mk", [[1, 128]], 0, -1, 128, -3)
-    iota(T.jm[:], "jm", [[0, 24], [1, 16]], 0, 0, NP, -2)
+    iota(T.pi[:], "pi", [[0, 4]], 0, 1, 4, -9, False)
+    iota(T.md16[:], "md16", [[1, 8], [0, 16]], 0, 0, 128, -9)
+    iota(T.oRi[:], "oRi", [[0, 4], [-8, 3]], 16, 0, 12, -8)
+    iota(T.mk[:], "mk", [[1, 128]], 0, -1, 128, -7)
+    iota(T.oKi[:], "oKi", [[1, 24]], 0, 0, 24, -4, False)
+    iota(T.jm[:, 0:128], "jm", [[0, 8], [1, 16]], 0, 0, 128, -5)
+    iota(T.cOw[:], "cOw", [[16, 24]], 128, 1, 24, -3)
+    iota(T.cD[:, 0:7], "cD", [[16, 7]], -1, 0, 7, -2)
+    gfill(T.Rs[:, 0:168], "Rs", 1, 168, -1)
+    gfill(T.Rs[:, 0:168:24], "Rs", 0, 7, -1)
     CQ, CQB, CS = [], [], []
-    for s, n, a, st in runs(prank + [rank]):
-        iota(T.cQ[:, 24 * s:24 * (s + n)], "cQ%d" % s, [[st, n], [0, 24]], a, 0, 24 * n, -4)
-        CQ.append("cQ%d" % s)
-    iota(T.oKi[:], "oKi", [[1, 24]], 0, 0, 24, 0, False)
-    iota(T.cOw[:], "cOw", [[16, 24]], 128, 1, 24, 0)
-    iota(T.cD[:, 0:168], "cD", [[16, 7], [0, 24]], -1, 0, 168, 0)
+    for k, v in enumerate(prank + [rank]):
+        act(T.cQ[:, 24 * k:24 * k + 24], "cQ%d" % k, T.bc[:, 0:24], ["one"], 24, -8, scale=0.0, bias=float(v))
+        CQ.append("cQ%d" % k)
     iota(T.NB[:], "NB", [[1, PWID]], SH, 0, PWID, 1, False)
     load("S", "ldC", lambda: [g.scalar.dma_start(T.NB[16 * k:16 * k + 16:4, LO:HI], T.nbr[:]) for k in range(8)], 8, [], ["NB"], 0.8, 3.5)
-    iota(T.K0[:], "K0", [[0, 24], [1, 5]], 0, 0, 120, 1)
-    iota(T.S1[:], "S1", [[4, 8], [1, 5]], -1, 0, 40, 1)
-    iota(T.S2[:], "S2", [[16, 8], [4, 5]], -4, -1, 40, 1)
-    iota(T.sC[:], "sC", [[16, 8], [0, 5]], 1, -1, 40, 1)
+    iota(T.S1[:], "S1", [[8, 8], [1, 6]], -1, 0, 48, 1)
+    iota(T.sA[:], "sA", [[32, 8], [4, 6]], -4, 0, 48, 1)
+    iota(T.sC[:, 1:49], "sC", [[32, 8], [0, 6]], 1, 0, 48, 1)
+    gfill(T.sC[:, 0:1], "sC0", 0, 1, 1)
     iota(T.Ms[:], "Ms", [[1, 8]], 0, 0, 8, 1)
-    iota(T.cD[:, 168:224], "cDB", [[16, 7], [0, 8]], -1, 0, 56, 4)
+    gfill(T.R1c[:], "R1c", -BIG, 144, 1)
+    gfill(T.R1c[:, 5:144:6], "R1c", BIG, 24, 1)
     for s, n, a, st in runs(prank + [rank]):
         iota(T.cQ[:, 192 + 8 * s:192 + 8 * (s + n)], "cQB%d" % s, [[st, n], [0, 8]], a, 0, 8 * n, 4)
         CQB.append("cQB%d" % s)
@@ -268,65 +274,75 @@ def rank_program(g, core, T, topo):
         CS.append("cS%d" % s)
 
     ones = T.bc[0:1, 0:128]
-    fill(T.bc[:, 0:128], "one", 1.0, 64, 0)
-    fill(T.Rs[:, 0:168], "Rs", 1.0, 168, 0)
-    fill(T.Rs[:, 0:168:24], "Rs", 0.0, 7, 0)
-    fill(T.bc[:, 128:512], "c1k", 1024.0, 192, 0)
-    gfill(T.W1[:, 0:112], "W1", -1024, 112, 1)
+    iota(T.W1[:, 0:112], "W1", [[0, 112]], NONE, 0, 112, 0, False)
     gfill(T.PW[:, 0:LO], "PW0", 0, 8, 2)
     gfill(T.PW[:, HI:PWID], "PW1", 0, 8, 2)
-    ts(T.pj[:, 0:1], "pj0", T.pi[:, 0:1], "pi", 15, None, A.bitwise_and, n=1, prio=0)
-    ts(T.pj[:, 1:2], "pj1", T.pi[:, 0:1], "pi", 4, None, A.arith_shift_right, n=1, prio=0)
-    ts(T.pj[:, 2:3], "pj2", T.pi[:, 0:1], "pi", 2, None, A.arith_shift_right, n=1, prio=0)
-    vop(lambda: V.tensor_copy(T.pf[:, 0:3], T.pj[:, 0:3]), ["pj0", "pj1", "pj2"], ["pf"], 3, 0)
-    p16, pg, p4 = T.pf[:, 0:1], T.pf[:, 1:2], T.pf[:, 2:3]
+    ts(T.pj[:, 0:1], "pj0", T.pi[:, 0:1], "pi", 15, None, A.bitwise_and, n=1, prio=-7)
+    ts(T.pj[:, 1:2], "pj1", T.pi[:, 0:1], "pi", 4, None, A.arith_shift_right, n=1, prio=-7)
+    ts(T.pj[:, 2:3], "pj2", T.pi[:, 0:1], "pi", 2, None, A.arith_shift_right, n=1, prio=-7)
+    vop(lambda: V.tensor_copy(T.pf[:, 0:3], T.pj[:, 0:3]), ["pj0", "pj1", "pj2"], ["pf"], 3, -7)
+    p16, pg, p4, p8, p32, pK = [T.pf[:, k:k + 1] for k in range(6)]
     oK, oE, oR, oB8 = T.oT[:, 0:24], T.oT[:, 24:48], T.oT[:, 48:60], T.oT[:, 64:68]
-    ts(oR, "oR", T.oRi[:], "oRi", p16, None, A.add, n=12, prio=0, extra=["pf"])
-    ts(T.G16[:], "G16", T.md16[:], "md16", pg, None, A.is_equal, n=128, prio=0, extra=["pf"])
-    ts(T.I16[:], "I16", T.mk[:], "mk", 0.0, None, A.is_equal, n=128, prio=0)
+    ts(oR, "oR", T.oRi[:], "oRi", p16, None, A.add, n=12, prio=-6, extra=["pf"])
+    ts(T.G16[:], "G16", T.md16[:], "md16", pg, None, A.is_equal, n=128, prio=-3, extra=["pf"])
+    ts(T.I16[:], "I16", T.mk[:], "mk", 0.0, None, A.is_equal, n=128, prio=-1)
     cp(T.If[:], "If", T.I16[:], "I16", 128, 2)
     ts(T.mk[:], "mk", T.mk[:], "mk", 0.0, -1.0, A.is_lt, A.mult, n=128, prio=0)
     tt(T.U16[:], "U16", T.mk[:], "mk", T.G16[:], "G16", A.mult, n=128, prio=0, f=2)
-    cp(T.cO16[:], "cO16", T.cOw[:], "cOw", 24, 0)
-    cp(oK, "oK", T.oKi[:], "oKi", 24, 0)
-    ts(T.m16[:], "m16", T.jm[:], "jm", p16, None, A.is_equal, n=NP, prio=0, extra=["pf"])
-    ts(T.G2k[:], "G2k", T.md16[:], "md16", pg, 2048.0, A.is_equal, A.mult, n=128, prio=0, extra=["pf"])
-    ts(T.Rd[:], "Rd", T.jm[:], "jm", 1.0, None, A.is_ge, n=NP, prio=0)
+    cp(T.cO16[:], "cO16", T.cOw[:], "cOw", 24, -1)
+    cp(oK, "oK", T.oKi[:], "oKi", 24, -1)
+    ts(T.m16[:, 0:128], "m16", T.jm[:], "jm", p16, None, A.is_equal, n=64, prio=-1, extra=["pf"])
+    act(T.m16[:, 128:256], "m16b", T.m16[:, 0:128], ["m16"], 128, -1)
+    act(T.m16[:, 256:384], "m16c", T.m16[:, 0:128], ["m16"], 128, -1)
+    M16 = ["m16", "m16b", "m16c"]
+    ts(T.G2k[:], "G2k", T.md16[:], "md16", pg, 2048.0, A.is_equal, A.mult, n=128, prio=-1, extra=["pf"])
+    gfill(T.scD[:, 0:1], "scD0", 0, 1, 0)
+    act(T.scC[:, 0:112], "scC", T.m16[:, 0:112], ["m16"], 112, 0, scale=-float(BIG))
+    act(T.scD[:, 1:112], "scD", T.m16[:, 0:111], ["m16"], 112, 0, scale=float(MID))
+    tt(T.scC[:, 0:112], "scC", T.scC[:, 0:112], "scC", T.scD[:], "scD", A.add, n=112, prio=0, f=2, extra=["scD0"])
+    act(T.scC[:, 112:192], "scCb", T.scC[:, 0:80], ["scC"], 80, 5)
 
-    def slots(oh, ohn, M, co, cqn, rkw, rkn, offs, offn, cdn, ro, rsn, su, sun, prio, cnt=None):
+    def slots(oh, ohn, M, co, cqn, rkw, rkn, offs, offn, rs, rsn, su, sun, prio, cnt=None):
         n7, n8 = 7 * M, 8 * M
-        cq, cd, rs = T.cQ[:, co:co + n8], T.cD[0:1, ro:ro + n7], T.Rs[:, ro:ro + n7]
-        sc, z1, z2 = T.scn, T.z1, T.z2
-        mm([((T.rB[:, n7:n8], T.I16[:], T.cO16[:, 0:M], True, True), M, 0),
-            ((T.rB[:, 0:n7], ones, cd, True, False), n7, 0)], ["I16", "cO16", "one", cdn], "rB", prio)
+        cq = T.cQ[:, co:co + n8]
+        z1, z2 = T.z1, T.z2
+        if cnt is None:
+            mm([((T.rB[:, n7:n8], T.I16[:], T.cO16[:, 0:M], True, True), M, 0)], ["I16", "cO16"], "rB", prio)
         vop(lambda: V.tensor_tensor(oh[:, 0:n8], rkw.indirect(offs), cq, A.is_equal), rkn + offn + cqn, [ohn], n8, prio, f=1.5)
-        l = [((T.rA[:, 0:n7], T.G16[:], oh[:, 0:n7], True, cnt is None), n7, 0)]
         if cnt is not None:
-            l.append(((T.rA[:, 0:n7:M], T.I16[:], cnt, False, True), 7, 0))
-        mm(l, ["G16", ohn] + (["I16", "cnt"] if cnt is not None else []), "rA", prio)
-        mm([((T.rB[:, 0:n7], T.U16[:], oh[:, 0:n7], False, True), n7, 0)], ["U16", ohn], "rB", prio)
-        vop(lambda: V.tensor_tensor_scan(sc[:, 0:n7], rs, T.rA[:, 0:n7], 0.0, A.mult, A.add), [rsn, "rA"], ["scn"], n7, prio)
+            mm([((T.rA[:, 0:n7], T.G16[:], oh[:, 0:n7], True, False), n7, 0), ((T.rA[:, 0:n7:M], T.I16[:], cnt, False, True), 7, 0)],
+               ["G16", ohn, "I16", "cnt"], "rA", prio)
+            mm([((T.rB[:, 0:n8], T.I1k[:], oh[:, 0:n8], True, False), n8, 0), ((T.rB[:, 0:n7], T.U16[:], oh[:, 0:n7], False, False), n7, 0),
+                ((T.rB[:, n7:n8], T.I16[:], T.cO16[:, 0:M], False, True), M, 0)], ["I1k", "U16", "I16", "cO16", ohn], "rB", prio)
+            vop(lambda: V.tensor_tensor_scan(T.scn[:, 0:n7], rs, T.rA[:, 0:n7], 0.0, A.mult, A.add), [rsn, "rA"], ["scn"], n7, prio)
+            vop(lambda: V.tensor_tensor(T.zz[:, 0:n8], T.scn[:, 0:n8], T.rB[:, 0:n8], A.add), ["scn", "scnz", "rB"], ["zz"], n8, prio)
+            h = n8 // 2
+            tt(T.mx[:, 0:h], "mx0", T.zz[:, 0:h], "zz", T.zz[:, h:n8], "zz", A.max, n=h, prio=prio)
+            tt(T.mx[:, 32:32 + h // 2], "mx1", T.mx[:, 0:h // 2], "mx0", T.mx[:, h // 2:h], "mx0", A.max, n=h // 2, prio=prio)
+            tt(T.mx[:, 48:48 + M], "mx2", T.mx[:, 32:32 + M], "mx1", T.mx[:, 32 + M:32 + 2 * M], "mx1", A.max, n=M, prio=prio)
+            return ts(su[:, 0:M], sun, T.mx[:, 48:48 + M], "mx2", -1024.0, None, A.add, n=M, prio=prio)
+        mm([((T.rA[:, 0:n7], T.G16[:], oh[:, 0:n7], True, False), n7, 0), ((T.rA[:, 0:n7:M], ones, T.cD[0:1, 0:7], False, True), 7, 0)],
+           ["G16", ohn, "one", "cD"], "rA", prio)
+        mm([((T.rB[:, 0:n7], T.U16[:], oh[:, 0:n7], True, True), n7, 0)], ["U16", ohn], "rB", prio)
+        sc = T.rA[:, 256:256 + n7]
+        vop(lambda: V.tensor_tensor_scan(sc, rs, T.rA[:, 0:n7], 0.0, A.mult, A.add), [rsn, "rA"], ["sc"], n7, prio)
         vop(lambda: V.tensor_tensor(z2[:, 0:n8], T.rB[:, 0:n8], oh[:, 0:n8], A.mult), ["rB", ohn], ["z2"], n8, prio)
-        vop(lambda: V.tensor_tensor(z1[:, 0:n7], sc[:, 0:n7], oh[:, 0:n7], A.mult), ["scn", ohn], ["z1"], n7, prio, f=2)
-        mm([((T.rA[:, 0:M], T.I16[:], z2[:, M * b:M * b + M], b == 0, False), M, 0) for b in range(8)], ["I16", "z2"], "rA", prio)
-        mm([((T.rA[:, 0:M], T.I16[:], z1[:, M * b:M * b + M], False, b == 6), M, 0) for b in range(7)], ["I16", "z1"], "rA", prio)
-        cp(su[:, 0:M], sun, T.rA[:, 0:M], "rA", M, prio)
+        vop(lambda: V.tensor_tensor(z1[:, 0:n7], sc, oh[:, 0:n7], A.mult), ["sc", "rA", ohn], ["z1"], n7, prio)
+        mm([((T.rB[:, 0:M], T.I16[:], z2[:, M * b:M * b + M], b == 0, False), M, 0) for b in range(8)], ["I16", "z2"], "rB", prio)
+        mm([((T.rB[:, 0:M], T.I16[:], z1[:, M * b:M * b + M], False, b == 6), M, 0) for b in range(7)], ["I16", "z1"], "rB", prio)
+        cp(su[:, 0:M], sun, T.rB[:, 0:M], "rB", M, prio)
 
-    def pack(xap, xn, tib, k, prio, off1k):
+    def pack(xap, xn, tib, tin, k, prio):
         n = 16 * k
-        if off1k:
-            mm([((T.rC[:, 0:n], ones, T.bc[0:1, 128:128 + n], True, False), n, 0)], ["one", "c1k"], "rC", prio)
-        vop(lambda: V.tensor_tensor(T.ex[:, 0:n], tib.indirect(T.oT[:, 0:k]), T.m16[:, 0:n], A.mult), ["ti", "oK", "m16"], ["ex"], n, prio, f=1.6)
-        mm([((T.rC[:, 0:n], T.G2k[:], T.ex[:, 0:n], not off1k, True), n, 0)], ["G2k", "ex"], "rC", prio)
+        vop(lambda: V.tensor_tensor(T.ex[:, 0:n], tib.indirect(T.oT[:, 0:k]), T.m16[:, 0:n], A.mult), [tin, "oK"] + M16, ["ex"], n, prio, f=1.6)
+        mm([((T.rC[:, 0:n], T.G2k[:], T.ex[:, 0:n], True, True), n, 0)], ["G2k", "ex"], "rC", prio)
         tt(T.PK[:, 0:n], "PK", T.rC[:, 0:n], "rC", xap, xn, A.add, n=n, prio=prio)
 
-    def decode(W, wn, yi, yin, tl, tln, msg, msgn, prio):
-        tt(T.dg[:], "dg", W[:, 0:112], wn, T.m16[:, 0:112], "m16", A.mult, n=112, prio=prio, f=2)
-        ts(yi[:], yin, W[:, 0:112], wn, 2047, None, A.bitwise_and, n=112, prio=prio)
-        vop(lambda: V.tensor_tensor_scan(T.sd[:], T.Rd[:, 0:112], T.dg[:], 0.0, A.mult, A.add), ["Rd", "dg"], ["sd"], 112, prio)
-        ts(msg[:, :, 0:16], msgn, yi[:], yin, -1024.0, None, A.add, n=112, prio=prio)
-        ts(tl[:, 0:7], tln, T.sd[:, 15:112:16], "sd", 11, None, A.arith_shift_right, n=7, prio=prio)
-        cp(msg[:, :, 16], msgn, tl[:, 0:7], tln, 7, prio)
+    def decode(W, wn, yi, yin, msg, msgn, prio):
+        vop(lambda: V.tensor_tensor_scan(T.sd[:], T.scC[:, 0:112], W[:, 0:112], 0.0, A.add, A.max), ["scC", wn], ["sd"], 112, prio)
+        ts(yi[:, :, 0:16], yin, W[:, 0:112], wn, 2047, None, A.bitwise_and, n=112, prio=prio)
+        ts(yi[:, :, 16], yin + "t", T.sd[:, 15:112:16], "sd", 11, 2047, A.arith_shift_right, A.bitwise_and, n=7, prio=prio)
+        cp(msg[:], msgn, yi[:], yin, 119, prio, extra=[yin + "t"])
 
     nloc = [0]
 
@@ -365,8 +381,8 @@ def rank_program(g, core, T, topo):
 
     def step(t, k, X, xn, w, wn, L, Ln, bK, bP, bL, prio, last=None, Lacc=None, Laccn=None):
         B = 3 if k == 24 else 1
-        m, kc = 40 * B, 8 * B
-        pr, pa, u, c, kp, p, re, e = [T[x + t] for x in ("pr", "pa", "u", "c", "k", "p", "re", "e")]
+        m, kc = 48 * B, 8 * B
+        pr, pa, u, kp, re, e = [T[x + t] for x in ("pr", "pa", "u", "k", "re", "e")]
         nm = lambda x: x + t
         part = lambda x, q: x + t + ("" if B == 1 else "_%d" % q)
         lo = 256 if bK == bL else 0
@@ -376,23 +392,25 @@ def rank_program(g, core, T, topo):
             add("S", lambda a=a, z=z: [S.activation(pa[:, 16 * a:16 * z], T.ND[:].indirect(w[:, a:z]), F.Copy)], ["ND", wn], [part("pa", q)],
                 0.1 + 1.8 * cy * 16 * (z - a), prio)
         for b in range(B):
-            mm([((T[bK][:, 40 * b:40 * b + 40], pr[:, 128 * b:128 * b + 128], T.S1[:], True, True), 40, 1)], [part("pr", b // 2), "S1"], bK, prio)
+            first = mm([((T[bK][:, 48 * b:48 * b + 48], pr[:, 128 * b:128 * b + 128], T.S1[:], True, True), 48, 1)],
+                       [part("pr", b // 2), "S1"], bK, prio)
         for b in range(B):
-            mm([((T[bP][:, 40 * b:40 * b + 40], pa[:, 128 * b:128 * b + 128], T.S2[:], True, True), 40, 1)], [part("pa", b // 2), "S2"], bP, prio)
+            second = mm([((T[bP][:, 48 * b:48 * b + 48], pa[:, 128 * b:128 * b + 128], T.S2[:], True, True), 48, 1)],
+                        [part("pa", b // 2), "S2"], bP, prio)
+        if B == 1:
+            tasks[second]["odeps"].add(first)
         Li, Lin = (L, Ln) if Lacc is None else (Lacc, Laccn)
         il = lambda: mm([((T[bL][:, lo:lo + kc], T.If[:], Li[:, 0:kc], True, False), kc, 1)], ["If", Lin], bL, prio)
         if bL != bK:
             il()
-        vop(lambda: V.tensor_tensor_scan(u[:, 1:m + 1], T.R1c[:, 0:m], T[bK][:, 0:m], 0.0, A.max, A.min), ["R1c", bK], [nm("u")], m, prio)
-        vop(lambda: V.tensor_tensor(c[:, 0:m], T[bK][:, 0:m], u[:, 0:m], A.is_lt), [bK, nm("u"), nm("u0")], [nm("c")], m, prio)
+        vop(lambda: V.tensor_tensor_scan(u[:, 1:m + 1], T[bK][:, 0:m], T.R1c[:, 0:m], 0.0, A.min, A.max), ["R1c", bK], [nm("u")], m, prio)
+        vop(lambda: V.tensor_tensor(kp[:, 0:m], T[bK][:, 0:m], u[:, 0:m], A.is_ge), [bK, nm("u"), nm("u0")], [nm("k")], m, prio)
         if bL == bK:
             il()
-        vop(lambda: V.tensor_tensor(kp[:, 0:m], T.K0[:, 0:m], c[:, 0:m], A.is_gt), ["K0", nm("c")], [nm("k")], m, prio, f=2)
-        vop(lambda: V.tensor_tensor(p[:, 0:m], T[bP][:, 0:m], c[:, 0:m], A.mult), [bP, nm("c")], [nm("p")], m, prio)
-        vop(lambda: V.tensor_tensor_scan(re[:, 0:m], kp[:, 0:m], p[:, 0:m], 0.0, A.mult, A.add), [nm("k"), nm("p")], [nm("re")], m, prio)
+        vop(lambda: V.tensor_tensor_scan(re[:, 0:m], T[bP][:, 0:m], kp[:, 0:m], 0.0, A.add, A.mult), [nm("k"), bP], [nm("re")], m, prio)
         for q, (a, z) in enumerate(((0, 16), (16, 24)) if B == 3 else ((0, 8),)):
             vop(lambda a=a, z=z: V.tensor_tensor(e[:, 16 * a:16 * z], re[:, 0:m].indirect(T.oT[:, 24 + a:24 + z]), T.m16[:, 16 * a:16 * z], A.mult),
-                [nm("re"), "oE", "m16"], [part("e", q)], 16 * (z - a), prio, f=1.6)
+                [nm("re"), "oE"] + M16, [part("e", q)], 16 * (z - a), prio, f=1.6)
         for b in range(B):
             mm([((T[bL][:, lo + 8 * b:lo + 8 * b + 8], e[:, 128 * b:128 * b + 128], T.Ms[:], False, b == B - 1), 8, 1)],
                [part("e", b // 2), "Ms"], bL, prio)
@@ -402,36 +420,42 @@ def rank_program(g, core, T, topo):
             ts(w[:, 0:k], wn, T[bL][:, lo:lo + k], bL, 0.0, float(HI), A.max, A.min, n=k, prio=prio)
             act(L[:, 0:kc], Ln, T[bL][:, lo:lo + kc], [bL], kc, prio)
 
-    ts(T.rk[:, 24:40], "rka", T.L0[:, 0:16], "L0", 10, None, A.arith_shift_right, prio=0)
-    ts(T.rk[:, 8:24], "rkb", T.L0[:, 8:24], "L0", 10, None, A.arith_shift_right, prio=0)
-    gfill(T.rk[:, 0:8], "rkz", -1, 8, 0)
-    gfill(T.rk[:, 40:48], "rkz2", -1, 8, 0)
-    RK = ["rka", "rkb", "rkz", "rkz2"]
+    ts(T.rk[:, 16:32], "rka", T.L0[:, 0:16], "L0", 10, None, A.arith_shift_right, prio=-4)
+    ts(T.rk[:, 0:16], "rkb", T.L0[:, 8:24], "L0", 10, None, A.arith_shift_right, prio=-4)
+    RK = ["rka", "rkb"]
+    slots(T.oh1, "oh1", 24, 0, CQ, T.rk[:, 0:32], RK, oR, ["oR"], T.Rs[:, 0:168], "Rs", T.su1, "su1", 0)
     ts(T.ti[:], "ti", T.L0[:], "L0", 1023, None, A.bitwise_and, prio=0)
-    slots(T.oh1, "oh1", 24, 0, CQ, T.rk[:], RK, oR, ["oR"], "cD", 0, "Rs", T.su1, "su1", 0)
-    pack(T.X[:], "X", T.ti[:], 24, 0, True)
+    ts(T.tf[:], "tf", T.ti[:], "ti", 0.5, None, A.add, prio=0)
+    pack(T.X[:], "X", T.tf[:], "tf", 24, 0)
     cp(T.W1[:].indirect(T.su1[:]), "W1", T.PK[:], "PK", NP, 0, extra=["su1"], f=3.5)
-    decode(T.W1, "W1", T.yi1, "yi1", T.tl1, "tl1", T.msg1, "msg1", 0)
+    decode(T.W1, "W1", T.yi1, "yi1", T.msg1, "msg1", 0)
     s1 = send(T.msg1, "msg1", "hq1", "land1", "rq1", True, 0)
 
-    ts(T.K0[:], "K0", T.K0[:], "K0", 1.0, None, A.is_ge, n=120, prio=2)
-    act(T.R1c[:], "R1c", T.K0[:], ["K0"], 120, 2, scale=-BIG)
-    ts(T.S1[:], "S1", T.S1[:], "S1", p4, None, A.is_equal, n=40, prio=2, extra=["pf"])
-    tt(T.S1[:], "S1", T.S1[:], "S1", T.K0[:, 0:40], "K0", A.mult, n=40, prio=2)
-    ts(T.S2[:], "S2", T.S2[:], "S2", 0.0, None, A.is_equal, n=40, prio=2)
-    ts(T.sC[:], "sC", T.sC[:], "sC", 0.0, None, A.is_equal, n=40, prio=2)
-    tt(T.S2[:], "S2", T.S2[:], "S2", T.sC[:], "sC", A.subtract, n=40, prio=2)
-    tt(T.S2[:], "S2", T.S2[:], "S2", T.K0[:, 0:40], "K0", A.mult, n=40, prio=2)
+    ts(p8, "p8", pg, "pf", 4.0, p4, A.mult, A.add, n=1, prio=2)
+    ts(p32, "p32", pg, "pf", 32.0, p16, A.mult, A.add, n=1, prio=2)
+    ts(T.S1[:], "S1", T.S1[:], "S1", p8, None, A.is_equal, n=48, prio=2, extra=["p8"])
+    ts(T.sA[:], "sA", T.sA[:], "sA", p32, None, A.is_equal, n=48, prio=2, extra=["p32"])
+    ts(T.sC[:, 1:49], "sC", T.sC[:, 1:49], "sC", p32, None, A.is_equal, n=48, prio=2, extra=["p32"])
+    fill(T.sC[:, 1:49:6], "sC", 0.0, 8, 2)
+    fill(T.sC[:, 6:49:6], "sC", 0.0, 8, 2)
+    tt(T.sC[:, 1:49], "sC", T.sA[:], "sA", T.sC[:, 1:49], "sC", A.subtract, n=48, prio=2)
+    tt(T.S2[:], "S2", T.sC[:, 0:48], "sC", T.sC[:, 1:49], "sC", A.subtract, n=48, prio=2, extra=["sC0"])
     ts(T.Ms[:], "Ms", T.Ms[:], "Ms", pg, None, A.is_equal, n=8, prio=2, extra=["pf"])
-    ts(oE, "oE", T.oKi[:], "oKi", 5.0, 4.0, A.mult, A.add, n=24, prio=2)
+    ts(oE, "oE", T.oKi[:], "oKi", 6.0, 5.0, A.mult, A.add, n=24, prio=2)
+    act(T.Rd[:, 0:128], "Rd", T.jm[:], ["jm"], 128, 5)
+    ts(T.Rd[:, 0:128], "Rd", T.Rd[:, 0:128], "Rd", 1.0, None, A.min, n=128, prio=5)
+    act(T.Rd[:, 128:256], "Rdb", T.Rd[:, 0:128], ["Rd"], 128, 5)
+    act(T.Rd[:, 256:384], "Rdc", T.Rd[:, 0:128], ["Rd"], 128, 5)
+    ts(T.I1k[:], "I1k", T.I16[:], "I16", 1024.0, None, A.mult, n=64, prio=4)
+    gfill(T.scn[:, 56:64], "scnz", 0, 8, 4)
     for t in ("O", "V", "R"):
-        gfill(T["u" + t][:, 0:1], "u0" + t, 0, 1, 2)
+        gfill(T["u" + t][:, 0:1], "u0" + t, BIG, 1, 2)
     for t in ("V", "R"):
         gfill(T["pr" + t][:, 112:128], "pr" + t, 0, 16, 2)
         gfill(T["pa" + t][:, 112:128], "pa" + t, 0, 16, 2)
     gfill(T.Lv[:, 7:8], "Lv", 0, 1, 2)
     gfill(T.Lv0[:, 7:8], "Lv0", 0, 1, 2)
-    cp(T.ND[:], "ND", T.NB[:], "NB", PWID, 3)
+    cp(T.ND[:], "ND", T.NB[:], "NB", PWID, 2)
     ts(T.Lo[:], "Lo", T.L0[:], "L0", float(-SH) - DEAD, None, A.add, prio=2)
     tt(T.Lo[:], "Lo", T.Lo[:], "Lo", T.oh1[:, 168:192], "oh1", A.mult, prio=2)
     ts(T.Lo[:], "Lo", T.Lo[:], "Lo", DEAD, None, A.add, prio=2)
@@ -439,9 +463,9 @@ def rank_program(g, core, T, topo):
     own = lambda pr: step("O", 24, T.X, "X", T.wO, "wO", T.Lo, "Lo", "oK", "oP", "oK", pr)
     own(P_O1)
 
-    def visitors(land, ln, out, outn, sem, sent):
-        add("V", lambda: [V.tensor_scalar(T.wv[:, 0:7], land[:, :, 16], 8.0, None, A.add)], [], ["wv", ln], 0.08, 0, [(sem, ARR)], (sent, FLY_REQ))
-        cp(T.Xv[:], "Xv", land[:, :, 0:16], ln, 112, 0)
+    def visitors(land, ln, out, outn, sem, sent, fly):
+        add("V", lambda: [V.tensor_scalar(T.wv[:, 0:7], land[:, :, 16], 8.0, None, A.add)], [], ["wv", ln], 0.08, 0, [(sem, ARR)], (sent, fly))
+        ts(T.Xv[:], "Xv", land[:, :, 0:16], ln, -1024.0, None, A.add, n=112, prio=0)
         add("V", lambda: [V.tensor_scalar(T.Lv0[:, 0:7], land[:, :, 16], 8.0, None, A.add)], [ln], ["Lv0"], 0.08, 1)
         act(T.Lv[:, 0:7], "Lv", T.Lv0[:, 0:7], ["Lv0"], 7, 1)
         a = (7, T.Xv, "Xv", T.wv, "wv", T.Lv, "Lv", "vK", "vP", "vL", 0)
@@ -450,16 +474,17 @@ def rank_program(g, core, T, topo):
         tt(T.Ld[:], "Ld", T.Lv[:], "Lv", T.Lv0[:], "Lv0", A.subtract, n=8, prio=0)
         step("V", *a, last=(out, outn), Lacc=T.Ld, Laccn="Ld")
 
-    visitors(T.land1, "land1", T.out1, "out1", "rq1", s1)
+    visitors(T.land1, "land1", T.out1, "out1", "rq1", s1, FLY[0])
     s2 = send(T.out1, "out1", "hp1", "rep1", "rp1", False, 0)
 
-    ts(T.sBv[:, 0:7], "sBv", T.tl1[:, 0:7], "tl1", -DEAD, None, A.add, n=7, prio=4)
+    ts(T.sBv[:, 0:7], "sBv", T.yi1[:, :, 16], "yi1t", -DEAD, None, A.add, n=7, prio=4)
     tt(T.sBv[:, 0:7], "sBv", T.sBv[:, 0:7], "sBv", T.cS[:, 0:7], CS[0], A.add, n=7, prio=4, extra=CS[1:])
-    ts(T.sBg[:, 0:7], "sBg", T.tl1[:, 0:7], "tl1", 0.0, None, A.is_ge, n=7, prio=4)
+    ts(T.sBg[:, 0:7], "sBg", T.yi1[:, :, 16], "yi1t", float(NT), None, A.is_lt, n=7, prio=4)
     tt(T.sBv[:, 0:7], "sBv", T.sBv[:, 0:7], "sBv", T.sBg[:, 0:7], "sBg", A.mult, n=7, prio=4)
     ts(T.sBv[:, 0:7], "sBv", T.sBv[:, 0:7], "sBv", DEAD, None, A.add, n=7, prio=4)
-    ts(T.xB[:], "xB", T.yi1[:], "yi1", -1024.0, None, A.add, n=112, prio=5)
-    gfill(T.W2[:, 0:112], "W2", -1024, 112, 3)
+    cp(T.yB[:], "yB", T.yi1[:, :, 0:16], "yi1", 112, 4)
+    ts(T.xB[:], "xB", T.yi1[:, :, 0:16], "yi1", -1024.0, None, A.add, n=112, prio=5)
+    gfill(T.W2[:, 0:112], "W2", NONE, 112, 3)
     gfill(T.Rs[:, 168:224], "RsB", 1, 56, 4)
     gfill(T.Rs[:, 168:224:8], "RsB", 0, 7, 4)
     gfill(T.rkB[:, 7:8], "rkB", rank, 1, 4)
@@ -470,33 +495,35 @@ def rank_program(g, core, T, topo):
     own(P_O2)
 
     RKC = (SH - 511.1875) / 1024.0
-    ts(T.rk[:, 24:40], "rka", T.Lo[:, 0:16], "Lo", 1.0 / 1024, RKC, A.mult, A.add, prio=P_A)
-    ts(T.rk[:, 8:24], "rkb", T.Lo[:, 8:24], "Lo", 1.0 / 1024, RKC, A.mult, A.add, prio=P_A)
+    ts(T.rk[:, 16:32], "rka", T.Lo[:, 0:16], "Lo", 1.0 / 1024, RKC, A.mult, A.add, prio=P_A)
+    ts(T.rk[:, 0:16], "rkb", T.Lo[:, 8:24], "Lo", 1.0 / 1024, RKC, A.mult, A.add, prio=P_A)
     ts(T.ci[:], "ci", T.Lo[:], "Lo", float(SH), None, A.add, prio=P_A)
     ts(T.ti[:], "ti", T.ci[:], "ci", 1023, None, A.bitwise_and, prio=P_A)
-    slots(T.ohA, "ohA", 24, 0, CQ, T.rk[:], RK, oR, ["oR"], "cD", 0, "Rs", T.suA, "suA", P_A)
-    cp(T.cnt[:, 0:7], "cnt", T.scn[:, 23:168:24], "scn", 7, P_A)
-    pack(T.X[:], "X", T.ti[:], 24, P_A, True)
+    ts(T.tf[:], "tf", T.ti[:], "ti", 0.5, None, A.add, prio=P_A)
+    slots(T.ohA, "ohA", 24, 0, CQ, T.rk[:, 0:32], RK, oR, ["oR"], T.Rs[:, 0:168], "Rs", T.suA, "suA", P_A)
+    cp(T.cnt[:, 0:7], "cnt", T.rA[:, 279:424:24], "rA", 7, P_A, extra=["sc"])
+    pack(T.X[:], "X", T.tf[:], "tf", 24, P_A)
     cp(T.W2[:].indirect(T.suA[:]), "W2", T.PK[:], "PK", NP, P_A, extra=["suA"], f=3.5)
 
-    vop(lambda: V.tensor_tensor(T.Lb[:, 0:7], T.sBv[:, 0:7], T.rep1[:, 0:7], A.add), ["sBv"], ["Lb"], 7, 0, [("rp1", ARR)], (s2, FLY_REP))
+    vop(lambda: V.tensor_tensor(T.Lb[:, 0:7], T.sBv[:, 0:7], T.rep1[:, 0:7], A.add), ["sBv"], ["Lb"], 7, 0, [("rp1", ARR)], (s2, FLY[1]))
     ts(T.rkB[:, 0:7], "rkB", T.Lb[:, 0:7], "Lb", 1.0 / 1024, RKC, A.mult, A.add, n=7, prio=0)
     ts(T.ci[:, 0:7], "ci", T.Lb[:, 0:7], "Lb", float(SH), None, A.add, n=7, prio=0)
     ts(T.ti[:, 0:7], "ti", T.ci[:, 0:7], "ci", 1023, None, A.bitwise_and, n=7, prio=0)
-    slots(T.ohA, "ohA", 8, 192, CQB, T.rkB[:], ["rkB"], oB8, ["oB8"], "cDB", 168, "RsB", T.suB, "suB", 0, cnt=T.cnt[:, 0:7])
-    pack(T.yi1[:], "yi1", T.ti[:, 0:8], 7, 0, False)
+    slots(T.ohA, "ohA", 8, 192, CQB, T.rkB[:], ["rkB"], oB8, ["oB8"], T.Rs[:, 168:224], "RsB", T.suB, "suB", 0, cnt=T.cnt[:, 0:7])
+    pack(T.yB[:], "yB", T.ti[:, 0:8], "ti", 7, 0)
     cp(T.W2[:].indirect(T.suB[:, 0:7]), "W2", T.PK[:, 0:112], "PK", 112, 0, extra=["suB"], f=3.5)
-    decode(T.W2, "W2", T.yi2, "yi2", T.tl2, "tl2", T.msg2, "msg2", 0)
+    decode(T.W2, "W2", T.yi2, "yi2", T.msg2, "msg2", 0)
     s3 = send(T.msg2, "msg2", "hq2", "land2", "rq2", True, 0)
 
     ts(T.wr[:, 0:7], "wr", T.Lb[:, 0:7], "Lb", 0.0, float(HI), A.max, A.min, n=7, prio=P_C)
     cp(T.Gf[:], "Gf", T.G16[:], "G16", 128, P_C)
     gfill(T.vW[:, 112:120], "vW", 0, 8, 4)
-    gfill(T.dW[:, 112:136], "dW", 0, 24, 4)
+    gfill(T.dW[:, 112:136], "dW0", 8192, 24, 4)
+    ts(pK, "pK", p16, "pf", 14.5, -float(MID), A.is_lt, A.mult, n=1, prio=5)
     for _ in range(3):
         step("R", 7, T.xB, "xB", T.wr, "wr", T.Lb, "Lb", "rA", "rB", "rC", P_R)
         own(P_O3)
-    visitors(T.land2, "land2", T.out2, "out2", "rq2", s3)
+    visitors(T.land2, "land2", T.out2, "out2", "rq2", s3, FLY[2])
     s4 = send(T.out2, "out2", "hp2", "rep2", "rp2", False, 0)
 
     ts(T.s1c[:], "s1c", T.su1[:], "su1", 112.0, None, A.min, prio=P_C)
@@ -504,27 +531,29 @@ def rank_program(g, core, T, topo):
     ts(T.smB[:, 0:7], "smB", T.suB[:, 0:7], "suB", 128.0, None, A.min, n=7, prio=P_C)
     ts(T.vB[:, 0:7], "vB", T.Lb[:, 0:7], "Lb", 8192.0, 256.0, A.add, A.mult, n=7, prio=P_C)
     tt(T.vB[:, 0:7], "vB", T.vB[:, 0:7], "vB", T.smB[:, 0:7], "smB", A.add, n=7, prio=P_C)
-    vop(lambda: V.tensor_tensor(T.exv[:], T.vB[:, 0:7].indirect(T.oT[:, 0:7]), T.m16[:, 0:112], A.mult), ["vB", "oK", "m16"], ["exv"], 112, P_C, f=1.6)
+    vop(lambda: V.tensor_tensor(T.exv[:], T.vB[:, 0:7].indirect(T.oT[:, 0:7]), T.m16[:, 0:112], A.mult), ["vB", "oK"] + M16, ["exv"], 112, P_C, f=1.6)
     mm([((T.rC[:, 0:112], T.Gf[:], T.exv[:], True, True), 112, 1)], ["Gf", "exv"], "rC", P_C)
     cp(T.vW[:, 0:112], "vW", T.rC[:, 0:112], "rC", 112, P_C)
-    vop(lambda: V.tensor_tensor(T.gv[:], T.vW[:].indirect(T.s1c[:]), T.m16[:], A.mult), ["vW", "s1c", "m16"], ["gv"], NP, P_C, f=1.6)
-    vop(lambda: V.tensor_tensor_scan(T.sv[:], T.Rd[:], T.gv[:], 0.0, A.mult, A.add), ["Rd", "gv"], ["sv"], NP, P_C)
+    vop(lambda: V.tensor_tensor(T.gv[:], T.vW[:].indirect(T.s1c[:]), T.m16[:], A.mult), ["vW", "s1c"] + M16, ["gv", "gvb"], NP, P_C, f=1.6)
+    vop(lambda: V.tensor_tensor_scan(T.sv[:], T.Rd[:], T.gv[:], 0.0, A.mult, A.add), ["Rd", "Rdb", "Rdc", "gv", "gvb"], ["sv", "svb"], NP, P_C)
     ts(T.vO[:], "vO", T.Lo[:], "Lo", 8192.0, 256.0, A.add, A.mult, prio=P_C)
     tt(T.vO[:], "vO", T.vO[:], "vO", T.smA[:], "smA", A.add, prio=P_C)
     tt(T.vO[:], "vO", T.vO[:], "vO", T.oh1[:, 168:192], "oh1", A.mult, prio=P_C)
-    tt(T.vt[:], "vt", T.vO[:], "vO", T.sv[:, 15:NP:16], "sv", A.add, prio=P_C)
+    tt(T.vt[:], "vt", T.vO[:], "vO", T.sv[:, 15:NP:16], "sv", A.add, prio=P_C, extra=["svb"])
     ts(T.ci[:], "ci", T.vt[:], "vt", 255, None, A.bitwise_and, prio=P_C)
     cp(T.tau[:], "tau", T.ci[:], "ci", 24, P_C)
     ts(T.vt[:], "vt", T.vt[:], "vt", 8, None, A.arith_shift_right, prio=P_C)
-    ts(T.Yb[:], "Yb", T.vt[:], "vt", float(SH - 8192), None, A.add, prio=P_C)
+    ts(T.Yb[:], "Yb", T.vt[:], "vt", float(SH - 16384), pK, A.add, A.add, prio=P_C, extra=["pK"])
 
-    vop(lambda: V.tensor_tensor(T.exv[:], T.rep2[:, 0:7].indirect(T.oT[:, 0:7]), T.m16[:, 0:112], A.mult), ["oK", "m16"], ["exv"], 112, 0,
-        [("rp2", ARR)], (s4, FLY_REP), f=1.6)
+    vop(lambda: V.tensor_tensor(T.exv[:], T.rep2[:, 0:7].indirect(T.oT[:, 0:7]), T.m16[:, 0:112], A.mult), ["oK"] + M16, ["exv"], 112, 0,
+        [("rp2", ARR)], (s4, FLY[3]), f=1.6)
     mm([((T.rC[:, 0:112], T.Gf[:], T.exv[:], True, True), 112, 1)], ["Gf", "exv"], "rC", 0)
-    cp(T.dW[:, 0:112], "dW", T.rC[:, 0:112], "rC", 112, 0)
-    vop(lambda: V.tensor_tensor(T.gv[:], T.dW[:].indirect(T.tau[:]), T.m16[:], A.mult), ["dW", "tau", "m16"], ["gv"], NP, 0, f=1.6)
-    vop(lambda: V.tensor_tensor_scan(T.sv[:], T.Rd[:], T.gv[:], 0.0, A.mult, A.add), ["Rd", "gv"], ["sv"], NP, 0)
-    tt(T.vO[:], "vO", T.sv[:, 15:NP:16], "sv", T.Yb[:], "Yb", A.add, prio=0)
+    ts(T.dW[:, 0:112], "dW", T.rC[:, 0:112], "rC", 8192.0, None, A.add, n=112, prio=0)
+    add("S", lambda: [S.activation(T.gv[:, 192:NP], T.dW[:].indirect(T.tau[:, 12:24]), F.Copy)], ["dW", "dW0", "tau"], ["gvb"], 0.4, 0)
+    vop(lambda: V.tensor_copy(T.gv[:, 0:192], T.dW[:].indirect(T.tau[:, 0:12])), ["dW", "dW0", "tau"], ["gv"], 192, 0, f=1.6)
+    for h, n in ((0, ""), (192, "b")):
+        vop(lambda h=h: V.tensor_tensor_scan(T.sv[:, h:h + 192], T.scC[:], T.gv[:, h:h + 192], 0.0, A.add, A.max), ["scC", "scCb", "gv" + n], ["sv" + n], 192, 0)
+    tt(T.vO[:], "vO", T.sv[:, 15:NP:16], "sv", T.Yb[:], "Yb", A.add, prio=0, extra=["svb"])
     load("Y", "st", lambda: [g.sync.dma_start(T.y[:], T.vO[:])], 1, ["vO"], [], 0.1, 0.0)
 
     order = plan(tasks)

from concourse.bass import DstId, RemoteDMATransfer
from concourse.mybir import AluOpType as A, ActivationFunctionType as F

NT, NP, NK = 1024, 384, 24
LO, HI, PWID = 8, 1032, 1040
DEAD = 7.375
MSG = 17
WIN = 640
BIG, MID = 8388608, 4194304
NONE = (1 << 21) + 1024
N_REL, ENG_HOP, ENG_OUT, ENG_DIR = 2, 4, 4, 2
PER = 4 // N_REL

_sb = {
    "X": ([128, NP], "int32"), "L0": ([128, NK], "int32"), "PW": ([128, PWID], "int32"), "NB": ([128, PWID], "int32"),
    "ND": ([128, PWID], "float32"), "Xv": ([128, 112], "float32"), "xB": ([128, 112], "float32"),
    "pi": ([128, 4], "int32"), "pj": ([128, 8], "int32"), "pf": ([128, 8], "float32"), "jm": ([128, 128], "bfloat16"), "x1": ([128, NK], "int32"),
    "mk": ([128, 128], "float32"), "md16": ([128, 128], "float32"), "m16": ([128, NP], "bfloat16"), "Rd": ([128, NP], "float32"),
    "G16": ([128, 128], "float16"), "G2k": ([128, 128], "float16"), "Gf": ([128, 128], "float32"),
    "U16": ([128, 128], "float16"), "I16": ([128, 128], "float16"), "If": ([128, 128], "float32"),
    "S1": ([128, 48], "float32"), "S2": ([128, 48], "float32"), "sA": ([128, 48], "float32"), "sC": ([128, 49], "float32"), "Ms": ([128, 8], "float32"),
    "R1c": ([128, 144], "float32"), "scC": ([128, 192], "float32"), "scD": ([128, 112], "float32"), "I1k": ([128, 128], "float16"),
    "oKi": ([128, NK], "int32"), "oRi": ([128, 12], "float32"), "oT": ([128, 72], "uint16"),
    "Rs": ([128, 224], "float32"), "cQ": ([128, 256], "float32"), "cD": ([128, 8], "bfloat16"), "bc": ([128, 128], "bfloat16"),
    "cOw": ([128, NK], "float32"), "cO16": ([128, NK], "float16"), "cS": ([128, 8], "float32"),
    "rk": ([128, 32], "int32"), "ci": ([128, NK], "int32"), "ti": ([128, NK], "int32"), "tf": ([128, NK], "float32"), "rkB": ([128, 8], "int32"),
    "oh1": ([128, 192], "float16"), "ohA": ([128, 192], "float16"), "ex": ([128, NP], "float16"),
    "scn": ([128, 64], "float32"), "zz": ([128, 64], "float32"), "mx": ([128, 56], "float32"),
    "z1": ([128, 168], "float16"), "z2": ([128, 192], "float16"), "cnt": ([128, 8], "float16"), "PK": ([128, NP], "int32"),
    "su1": ([128, NK], "uint16"), "suA": ([128, NK], "uint16"), "suB": ([128, 8], "uint16"),
    "W1": ([128, WIN], "int32"), "W2": ([128, WIN], "int32"),
    "sd": ([128, 112], "int32"), "yi1": ([128, 7, MSG], "int32"), "yi2": ([128, 7, MSG], "int32"), "yB": ([128, 112], "int32"),
    "msg1": ([128, 7, MSG], "float16"), "msg2": ([128, 7, MSG], "float16"),
    "land1": ([128, 7, MSG], "float16"), "land2": ([128, 7, MSG], "float16"),
    "sBv": ([128, 8], "float32"), "sBg": ([128, 8], "float32"),
    "out1": ([128, 8], "float32"), "out2": ([128, 8], "float32"), "rep1": ([128, 8], "float32"), "rep2": ([128, 8], "float32"),
    "Lo": ([128, NK], "float32"), "wO": ([128, NK], "uint16"), "Lv": ([128, 8], "float32"), "Lv0": ([128, 8], "float32"),
    "Ld": ([128, 8], "float32"), "wv": ([128, 8], "uint16"), "Lb": ([128, 8], "float32"), "wr": ([128, 8], "uint16"),
    "smA": ([128, NK], "float32"), "smB": ([128, 8], "float32"), "vB": ([128, 8], "float32"), "exv": ([128, 112], "float32"),
    "vW": ([128, 120], "float32"), "s1c": ([128, NK], "uint16"), "gv": ([128, NP], "float32"), "sv": ([128, NP], "float32"),
    "vO": ([128, NK], "float32"), "vt": ([128, NK], "int32"), "tau": ([128, NK], "uint16"),
    "Yb": ([128, NK], "float32"), "dW": ([128, 136], "float32"),
    "hq1": ([128, PER, MSG], "float16"), "hq2": ([128, PER, MSG], "float16"), "hp1": ([128, PER], "float32"), "hp2": ([128, PER], "float32"),
}
for _t, _n in (("O", 384), ("V", 128), ("R", 128)):
    _m = _n // 128 * 48
    for _b, _w in (("pr", _n), ("pa", _n), ("u", _m + 8), ("k", _m), ("re", _m), ("e", _n)):
        _sb[_b + _t] = ([128, _w], "float32")
SCRATCH = {_k: ("sbuf", _v[0], _v[1]) for _k, _v in _sb.items()}
PSUM = ("oK", "oP", "vK", "vP", "vL", "rA", "rB", "rC")
for _k in PSUM:
    SCRATCH[_k] = ("psum", [128, 512], "float32")
SEMAPHORES = ["sV", "sS", "sT", "sG", "ldA", "ldP", "ldB", "ldC", "st", "rq1", "rq2", "rp1", "rp2", "hq1", "hq2", "hp1", "hp2", "loc"]

FLY = (9, 6.5, 6, 5)
WAKE, SLACK, SLACK2 = 0.1, 0.1, 0.1
P_O1, P_O2, P_A, P_O3, P_R, P_C = 2, 2, 1, 5, 4, 4


def wiring(T, topo, core):
    others = [c for c in T.cores if c != core]
    cross = [c for c in others if not topo.may_write(core, c)]
    direct = [c for c in others if topo.may_write(core, c)]
    rel = [c for c in topo.cores_of(core) if c not in T.cores and all(topo.may_write(c, d) for d in cross)]
    rel.sort(key=lambda c: (topo.die(c) != topo.die(core), c))
    return cross, direct, rel[:N_REL]


def emask(engs):
    return sum(1 << e for e in engs)


def place_of(T, topo, owner, dst):
    cross, direct, rel = wiring(T, topo, dst)
    return (cross + direct).index(owner)


def relay_program(g, core, T, topo, owner):
    cross, direct, rel = wiring(T, topo, owner)
    k = rel.index(core)
    dsts = cross[PER * k:PER * k + PER]
    n = 0
    for src, dname, sem_out, req in (("hq1", "land1", "rq1", True), ("hp1", "rep1", "rp1", False),
                                     ("hq2", "land2", "rq2", True), ("hp2", "rep2", "rp2", False)):
        g.wait_ge(T.sem[src], ENG_HOP)
        trs = []
        for i, d in enumerate(dsts):
            rid, pid = topo.addr(d, core)
            es = topo.engines(core, d)[ENG_OUT * i:ENG_OUT * i + ENG_OUT]
            at = place_of(T, topo, owner, d)
            if req:
                s_ap, d_ap = T[src][:, i, :], T[dname][:, at, :]
            else:
                s_ap, d_ap = T[src][:, i:i + 1], T[dname][:, at:at + 1]
            trs.append(RemoteDMATransfer(dst_ids=[DstId(rid=rid, pnc=pid)], dma_engine_mask=emask(es), remote_sem=T.sem[sem_out],
                                         src=s_ap, dst=d_ap))
            n += len(es)
        g.remote_dma_fused(trs, local_sem=T.sem.loc)
    g.wait_ge(T.sem.loc, n)


def plan(tasks):
    n = len(tasks)
    fin, free, order, ready = {}, {}, {}, {}
    pre = [t["deps"] | t["odeps"] | ({t["aft"][0]} if t["aft"] else set()) for t in tasks]
    pend = [len(x) for x in pre]
    succ = [[] for _ in tasks]
    for i, x in enumerate(pre):
        for d in x:
            succ[d].append(i)
    tail = [0.0] * n
    for i in range(n - 1, -1, -1):
        tail[i] = tasks[i]["cost"] + WAKE + max([0.0] + [tail[x] for x in succ[i] if tasks[x]["prio"] <= tasks[i]["prio"]])

    def enter(i):
        t = tasks[i]
        e = max([0.0] + [fin[d] + WAKE for d in t["deps"]] + [fin[d] for d in t["odeps"]])
        if t["aft"]:
            e = max(e, fin[t["aft"][0]] + t["aft"][1])
        ready.setdefault(t["q"], {})[i] = e
    for i in range(n):
        if pend[i] == 0:
            enter(i)
    while len(fin) < n:
        m, q = min((max(free.get(q, 0.0), min(l.values())), q) for q, l in ready.items() if l)
        l, fr = ready[q], free.get(q, 0.0)
        st = {i: max(fr, e) for i, e in l.items()}
        pick = min(l, key=lambda i: (tasks[i]["prio"], max(st[i] - m - SLACK, 0.0), -tail[i], i))
        if st[pick] > m + SLACK:
            fits = [i for i in l if st[i] + tasks[i]["cost"] <= st[pick] + SLACK2]
            now = [i for i in fits if st[i] <= m + SLACK]
            if now:
                pick = min(now, key=lambda i: (tasks[i]["prio"], -tail[i], i))
            elif fits:
                pick = min(fits, key=lambda i: (st[i], tasks[i]["prio"], i))
        fin[pick] = st[pick] + tasks[pick]["cost"]
        free[q] = fin[pick]
        fin[pick] += tasks[pick]["lat"]
        order.setdefault(q, []).append(pick)
        del l[pick]
        for x in succ[pick]:
            pend[x] -= 1
            if pend[x] == 0:
                enter(x)
    return order


def runs(v):
    out, i = [], 0
    while i < len(v):
        j, st = i + 1, (v[i + 1] - v[i] if i + 1 < len(v) else 0)
        while j < len(v) and v[j] - v[j - 1] == st:
            j += 1
        out.append((i, j - i, v[i], st if j - i > 1 else 0))
        i = j
    return out


def rank_program(g, core, T, topo):
    rank = T.rank_of(core)
    if rank is None:
        for c in T.cores:
            if c in topo.cores_of(core) and core in wiring(T, topo, c)[2]:
                relay_program(g, core, T, topo, c)
        return
    cross, direct, rel = wiring(T, topo, core)
    prank = [T.cores.index(c) for c in cross + direct]
    base = NT * rank
    SH = base - LO
    tasks, wr, rd = [], {}, {}
    V, S, E = g.vector, g.scalar, g.tensor
    cy = 0.00083

    def add(q, fn, reads, writes, cost, prio=1, ext=(), aft=None):
        i = len(tasks)
        deps, odeps = set(), set()
        for b in reads:
            if b in wr:
                deps.add(wr[b])
            if b in PSUM:
                deps.update(x for x in rd.get(b, ()) if tasks[x]["q"] != q)
        for b in writes:
            if b in wr:
                (odeps if q == "T" and tasks[wr[b]]["q"] == "T" else deps).add(wr[b])
            deps.update(rd.get(b, ()))
        tasks.append(dict(q=q, fn=fn, deps=deps, odeps=odeps, cost=cost, prio=prio, ext=tuple(ext), aft=aft, dma=None, lat=0.0))
        for b in reads:
            rd.setdefault(b, []).append(i)
        for b in writes:
            wr[b] = i
            rd[b] = []
        return i

    def vop(fn, reads, writes, n, prio=1, ext=(), aft=None, f=1.0):
        return add("V", lambda: [fn()], reads, writes, (0.02 if f == int(f) else 0.07) + 1.2 * cy * max(64, n * f), prio, ext, aft)

    def ts(out, on, in0, inn, s1, s2, op0, op1=None, n=24, prio=1, ext=(), aft=None, extra=()):
        if op1 is None:
            return vop(lambda: V.tensor_scalar(out, in0, s1, None, op0), [inn] + list(extra), [on], n, prio, ext, aft)
        return vop(lambda: V.tensor_scalar(out, in0, s1, s2, op0, op1), [inn] + list(extra), [on], n, prio, ext, aft)

    def tt(out, on, in0, n0, in1, n1, op, n=24, prio=1, ext=(), aft=None, extra=(), f=1.0):
        return vop(lambda: V.tensor_tensor(out, in0, in1, op), [n0, n1] + list(extra), [on], n, prio, ext, aft, f)

    def cp(out, on, in_, inn, n=24, prio=1, extra=(), f=1.0):
        return vop(lambda: V.tensor_copy(out, in_), [inn] + list(extra), [on], n, prio, f=f)

    def fill(ap, on, v, n, prio=1):
        return vop(lambda: V.memset(ap, v), [], [on], n, prio)

    def act(out, on, in_, inn, n, prio=1, **kw):
        return add("S", lambda: [S.activation(out, in_, F.Copy, **kw)], inn, [on], 0.03 + 1.2 * cy * max(64, n), prio)

    def iota(ap, on, pat, b, ch, n, prio=1, fl=True):
        if fl:
            return add("G", lambda: [g.iota(ap, pat, b, ch, allow_small_or_imprecise_dtypes=True)], [], [on], 0.15 + 2.2 * cy * n, prio)
        return add("G", lambda: [g.iota(ap, pat, b, ch)], [], [on], 0.15 + 2.2 * cy * n, prio)

    def gfill(ap, on, v, n, prio=1):
        return iota(ap, on, [[0, n]], v, 0, n, prio)

    def mm(lst, reads, bank, prio=1):
        c = sum((0.03 + 0.0008 * max(64, n) * (4 if f4 else 1)) for (_, n, f4) in lst)
        return add("T", lambda: [E.matmul(*a) for (a, n, f4) in lst], reads, [bank], c, prio)

    loads = {}

    def load(q, sem, fn, cnt, deps, writes, cost, lat, prio=0):
        i = add(q, fn, deps, writes, cost, prio)
        tasks[i]["dma"] = sem
        tasks[i]["lat"] = lat
        loads[sem] = loads.get(sem, 0) + 16 * cnt
        return i

    def ld_pts(q, fs):
        return [q.dma_start(T.X[4 * f + i:128:16, :], T.pts[i:24:3, :]) for f in fs for i in range(3)]

    fill(T.bc[:, 0:128], "one", 1.0, 64, -10)
    fill(T.x1[:], "x1", 1, NK, -9)
    load("Y", "ldA", lambda: [g.sync.dma_start(T.L0[:], T.tet0[:])], 1, [], ["L0"], 0.1, 2.0, -9)
    load("Y", "ldP", lambda: ld_pts(g.sync, (0, 1)) + [g.sync.dma_start(T.X[4 * f + 3:128:16, :], T.x1[:]) for f in range(4)],
         10, ["x1"], ["Xa"], 1.0, 2.0)
    load("S", "ldP", lambda: ld_pts(g.scalar, (2, 3)), 6, [], ["X"], 0.6, 2.5)
    load("Y", "ldB", lambda: [g.sync.dma_start(T.PW[16 * k:16 * k + 16, LO:HI], T.planes[:]) for k in range(8)], 8, [], ["PW"], 0.8, 4.0)

    iota(T.pi[:], "pi", [[0, 4]], 0, 1, 4, -9, False)
    iota(T.md16[:], "md16", [[1, 8], [0, 16]], 0, 0, 128, -9)
    iota(T.oRi[:], "oRi", [[0, 4], [-8, 3]], 16, 0, 12, -8)
    iota(T.mk[:], "mk", [[1, 128]], 0, -1, 128, -7)
    iota(T.oKi[:], "oKi", [[1, 24]], 0, 0, 24, -4, False)
    iota(T.jm[:, 0:128], "jm", [[0, 8], [1, 16]], 0, 0, 128, -5)
    iota(T.cOw[:], "cOw", [[16, 24]], 128, 1, 24, -3)
    iota(T.cD[:, 0:7], "cD", [[16, 7]], -1, 0, 7, -2)
    gfill(T.Rs[:, 0:168], "Rs", 1, 168, -1)
    gfill(T.Rs[:, 0:168:24], "Rs", 0, 7, -1)
    CQ, CQB, CS = [], [], []
    for k, v in enumerate(prank + [rank]):
        act(T.cQ[:, 24 * k:24 * k + 24], "cQ%d" % k, T.bc[:, 0:24], ["one"], 24, -8, scale=0.0, bias=float(v))
        CQ.append("cQ%d" % k)
    iota(T.NB[:], "NB", [[1, PWID]], SH, 0, PWID, 1, False)
    load("S", "ldC", lambda: [g.scalar.dma_start(T.NB[16 * k:16 * k + 16:4, LO:HI], T.nbr[:]) for k in range(8)], 8, [], ["NB"], 0.8, 3.5)
    iota(T.S1[:], "S1", [[8, 8], [1, 6]], -1, 0, 48, 1)
    iota(T.sA[:], "sA", [[32, 8], [4, 6]], -4, 0, 48, 1)
    iota(T.sC[:, 1:49], "sC", [[32, 8], [0, 6]], 1, 0, 48, 1)
    gfill(T.sC[:, 0:1], "sC0", 0, 1, 1)
    iota(T.Ms[:], "Ms", [[1, 8]], 0, 0, 8, 1)
    gfill(T.R1c[:], "R1c", -BIG, 144, 1)
    gfill(T.R1c[:, 5:144:6], "R1c", BIG, 24, 1)
    for s, n, a, st in runs(prank + [rank]):
        iota(T.cQ[:, 192 + 8 * s:192 + 8 * (s + n)], "cQB%d" % s, [[st, n], [0, 8]], a, 0, 8 * n, 4)
        CQB.append("cQB%d" % s)
    for s, n, a, st in runs(prank):
        iota(T.cS[:, s:s + n], "cS%d" % s, [[NT * st, n]], NT * a - SH, 0, n, 4)
        CS.append("cS%d" % s)

    ones = T.bc[0:1, 0:128]
    iota(T.W1[:, 0:112], "W1", [[0, 112]], NONE, 0, 112, 0, False)
    gfill(T.PW[:, 0:LO], "PW0", 0, 8, 2)
    gfill(T.PW[:, HI:PWID], "PW1", 0, 8, 2)
    ts(T.pj[:, 0:1], "pj0", T.pi[:, 0:1], "pi", 15, None, A.bitwise_and, n=1, prio=-7)
    ts(T.pj[:, 1:2], "pj1", T.pi[:, 0:1], "pi", 4, None, A.arith_shift_right, n=1, prio=-7)
    ts(T.pj[:, 2:3], "pj2", T.pi[:, 0:1], "pi", 2, None, A.arith_shift_right, n=1, prio=-7)
    vop(lambda: V.tensor_copy(T.pf[:, 0:3], T.pj[:, 0:3]), ["pj0", "pj1", "pj2"], ["pf"], 3, -7)
    p16, pg, p4, p8, p32, pK = [T.pf[:, k:k + 1] for k in range(6)]
    oK, oE, oR, oB8 = T.oT[:, 0:24], T.oT[:, 24:48], T.oT[:, 48:60], T.oT[:, 64:68]
    ts(oR, "oR", T.oRi[:], "oRi", p16, None, A.add, n=12, prio=-6, extra=["pf"])
    ts(T.G16[:], "G16", T.md16[:], "md16", pg, None, A.is_equal, n=128, prio=-3, extra=["pf"])
    ts(T.I16[:], "I16", T.mk[:], "mk", 0.0, None, A.is_equal, n=128, prio=-1)
    cp(T.If[:], "If", T.I16[:], "I16", 128, 2)
    ts(T.mk[:], "mk", T.mk[:], "mk", 0.0, -1.0, A.is_lt, A.mult, n=128, prio=0)
    tt(T.U16[:], "U16", T.mk[:], "mk", T.G16[:], "G16", A.mult, n=128, prio=0, f=2)
    cp(T.cO16[:], "cO16", T.cOw[:], "cOw", 24, -1)
    cp(oK, "oK", T.oKi[:], "oKi", 24, -1)
    ts(T.m16[:, 0:128], "m16", T.jm[:], "jm", p16, None, A.is_equal, n=64, prio=-1, extra=["pf"])
    act(T.m16[:, 128:256], "m16b", T.m16[:, 0:128], ["m16"], 128, -1)
    act(T.m16[:, 256:384], "m16c", T.m16[:, 0:128], ["m16"], 128, -1)
    M16 = ["m16", "m16b", "m16c"]
    ts(T.G2k[:], "G2k", T.md16[:], "md16", pg, 2048.0, A.is_equal, A.mult, n=128, prio=-1, extra=["pf"])
    gfill(T.scD[:, 0:1], "scD0", 0, 1, 0)
    act(T.scC[:, 0:112], "scC", T.m16[:, 0:112], ["m16"], 112, 0, scale=-float(BIG))
    act(T.scD[:, 1:112], "scD", T.m16[:, 0:111], ["m16"], 112, 0, scale=float(MID))
    tt(T.scC[:, 0:112], "scC", T.scC[:, 0:112], "scC", T.scD[:], "scD", A.add, n=112, prio=0, f=2, extra=["scD0"])
    act(T.scC[:, 112:192], "scCb", T.scC[:, 0:80], ["scC"], 80, 5)

    def slots(oh, ohn, M, co, cqn, rkw, rkn, offs, offn, rs, rsn, su, sun, prio, cnt=None):
        n7, n8 = 7 * M, 8 * M
        cq = T.cQ[:, co:co + n8]
        z1, z2 = T.z1, T.z2
        if cnt is None:
            mm([((T.rB[:, n7:n8], T.I16[:], T.cO16[:, 0:M], True, True), M, 0)], ["I16", "cO16"], "rB", prio)
        vop(lambda: V.tensor_tensor(oh[:, 0:n8], rkw.indirect(offs), cq, A.is_equal), rkn + offn + cqn, [ohn], n8, prio, f=1.5)
        if cnt is not None:
            mm([((T.rA[:, 0:n7], T.G16[:], oh[:, 0:n7], True, False), n7, 0), ((T.rA[:, 0:n7:M], T.I16[:], cnt, False, True), 7, 0)],
               ["G16", ohn, "I16", "cnt"], "rA", prio)
            mm([((T.rB[:, 0:n8], T.I1k[:], oh[:, 0:n8], True, False), n8, 0), ((T.rB[:, 0:n7], T.U16[:], oh[:, 0:n7], False, False), n7, 0),
                ((T.rB[:, n7:n8], T.I16[:], T.cO16[:, 0:M], False, True), M, 0)], ["I1k", "U16", "I16", "cO16", ohn], "rB", prio)
            vop(lambda: V.tensor_tensor_scan(T.scn[:, 0:n7], rs, T.rA[:, 0:n7], 0.0, A.mult, A.add), [rsn, "rA"], ["scn"], n7, prio)
            vop(lambda: V.tensor_tensor(T.zz[:, 0:n8], T.scn[:, 0:n8], T.rB[:, 0:n8], A.add), ["scn", "scnz", "rB"], ["zz"], n8, prio)
            h = n8 // 2
            tt(T.mx[:, 0:h], "mx0", T.zz[:, 0:h], "zz", T.zz[:, h:n8], "zz", A.max, n=h, prio=prio)
            tt(T.mx[:, 32:32 + h // 2], "mx1", T.mx[:, 0:h // 2], "mx0", T.mx[:, h // 2:h], "mx0", A.max, n=h // 2, prio=prio)
            tt(T.mx[:, 48:48 + M], "mx2", T.mx[:, 32:32 + M], "mx1", T.mx[:, 32 + M:32 + 2 * M], "mx1", A.max, n=M, prio=prio)
            return ts(su[:, 0:M], sun, T.mx[:, 48:48 + M], "mx2", -1024.0, None, A.add, n=M, prio=prio)
        mm([((T.rA[:, 0:n7], T.G16[:], oh[:, 0:n7], True, False), n7, 0), ((T.rA[:, 0:n7:M], ones, T.cD[0:1, 0:7], False, True), 7, 0)],
           ["G16", ohn, "one", "cD"], "rA", prio)
        mm([((T.rB[:, 0:n7], T.U16[:], oh[:, 0:n7], True, True), n7, 0)], ["U16", ohn], "rB", prio)
        sc = T.rA[:, 256:256 + n7]
        vop(lambda: V.tensor_tensor_scan(sc, rs, T.rA[:, 0:n7], 0.0, A.mult, A.add), [rsn, "rA"], ["sc"], n7, prio)
        vop(lambda: V.tensor_tensor(z2[:, 0:n8], T.rB[:, 0:n8], oh[:, 0:n8], A.mult), ["rB", ohn], ["z2"], n8, prio)
        vop(lambda: V.tensor_tensor(z1[:, 0:n7], sc, oh[:, 0:n7], A.mult), ["sc", "rA", ohn], ["z1"], n7, prio)
        mm([((T.rB[:, 0:M], T.I16[:], z2[:, M * b:M * b + M], b == 0, False), M, 0) for b in range(8)], ["I16", "z2"], "rB", prio)
        mm([((T.rB[:, 0:M], T.I16[:], z1[:, M * b:M * b + M], False, b == 6), M, 0) for b in range(7)], ["I16", "z1"], "rB", prio)
        cp(su[:, 0:M], sun, T.rB[:, 0:M], "rB", M, prio)

    def pack(xap, xn, tib, tin, k, prio):
        n = 16 * k
        vop(lambda: V.tensor_tensor(T.ex[:, 0:n], tib.indirect(T.oT[:, 0:k]), T.m16[:, 0:n], A.mult), [tin, "oK"] + M16, ["ex"], n, prio, f=1.6)
        mm([((T.rC[:, 0:n], T.G2k[:], T.ex[:, 0:n], True, True), n, 0)], ["G2k", "ex"], "rC", prio)
        tt(T.PK[:, 0:n], "PK", T.rC[:, 0:n], "rC", xap, xn, A.add, n=n, prio=prio)

    def decode(W, wn, yi, yin, msg, msgn, prio):
        vop(lambda: V.tensor_tensor_scan(T.sd[:], T.scC[:, 0:112], W[:, 0:112], 0.0, A.add, A.max), ["scC", wn], ["sd"], 112, prio)
        ts(yi[:, :, 0:16], yin, W[:, 0:112], wn, 2047, None, A.bitwise_and, n=112, prio=prio)
        ts(yi[:, :, 16], yin + "t", T.sd[:, 15:112:16], "sd", 11, 2047, A.arith_shift_right, A.bitwise_and, n=7, prio=prio)
        cp(msg[:], msgn, yi[:], yin, 119, prio, extra=[yin + "t"])

    nloc = [0]

    def send(src, srcn, hname, dname, sem, req, prio):
        def fn():
            own8 = topo.engines(core, direct[0])
            alle = topo.engines(core, rel[0])
            hop = [e for e in alle if e not in own8]
            if len(hop) < ENG_HOP * N_REL:
                hop = hop + [e for e in alle if e in own8]
            trs = []
            for k, r in enumerate(rel):
                rid, pid = topo.addr(r, core)
                s_ap = src[:, PER * k:PER * k + PER, :] if req else src[:, PER * k:PER * k + PER]
                es = hop[ENG_HOP * k:ENG_HOP * k + ENG_HOP]
                trs.append(RemoteDMATransfer(dst_ids=[DstId(rid=rid, pnc=pid)], dma_engine_mask=emask(es), remote_sem=T.sem[hname],
                                             src=s_ap, dst=T[hname][:]))
                nloc[0] += len(es)
            g.remote_dma_fused(trs, local_sem=T.sem.loc)
            trs = []
            for k, d in enumerate(direct):
                rid, pid = topo.addr(d, core)
                es = topo.engines(core, d)[ENG_DIR * k:ENG_DIR * k + ENG_DIR]
                b, at = len(cross) + k, place_of(T, topo, core, d)
                if req:
                    s_ap, d_ap = src[:, b, :], T[dname][:, at, :]
                else:
                    s_ap, d_ap = src[:, b:b + 1], T[dname][:, at:at + 1]
                trs.append(RemoteDMATransfer(dst_ids=[DstId(rid=rid, pnc=pid)], dma_engine_mask=emask(es), remote_sem=T.sem[sem],
                                             src=s_ap, dst=d_ap))
                nloc[0] += len(es)
            g.remote_dma_fused(trs, local_sem=T.sem.loc)
            return []
        return add("G", fn, [srcn], [], 1.0, prio)
    ARR = ENG_OUT * len(cross) + ENG_DIR * len(direct)

    def step(t, k, X, xn, w, wn, L, Ln, bK, bP, bL, prio, last=None, Lacc=None, Laccn=None):
        B = 3 if k == 24 else 1
        m, kc = 48 * B, 8 * B
        pr, pa, u, kp, re, e = [T[x + t] for x in ("pr", "pa", "u", "k", "re", "e")]
        nm = lambda x: x + t
        part = lambda x, q: x + t + ("" if B == 1 else "_%d" % q)
        lo = 256 if bK == bL else 0
        for q, (a, z) in enumerate(((0, 16), (16, 24)) if B == 3 else ((0, k),)):
            vop(lambda a=a, z=z: V.tensor_tensor(pr[:, 16 * a:16 * z], T.PW[:].indirect(w[:, a:z]), X[:, 16 * a:16 * z], A.mult),
                ["PW", "PW0", "PW1", wn, xn], [part("pr", q)], 16 * (z - a), prio, f=1.6)
            add("S", lambda a=a, z=z: [S.activation(pa[:, 16 * a:16 * z], T.ND[:].indirect(w[:, a:z]), F.Copy)], ["ND", wn], [part("pa", q)],
                0.1 + 1.8 * cy * 16 * (z - a), prio)
        for b in range(B):
            first = mm([((T[bK][:, 48 * b:48 * b + 48], pr[:, 128 * b:128 * b + 128], T.S1[:], True, True), 48, 1)],
                       [part("pr", b // 2), "S1"], bK, prio)
        for b in range(B):
            second = mm([((T[bP][:, 48 * b:48 * b + 48], pa[:, 128 * b:128 * b + 128], T.S2[:], True, True), 48, 1)],
                        [part("pa", b // 2), "S2"], bP, prio)
        if B == 1:
            tasks[second]["odeps"].add(first)
        Li, Lin = (L, Ln) if Lacc is None else (Lacc, Laccn)
        il = lambda: mm([((T[bL][:, lo:lo + kc], T.If[:], Li[:, 0:kc], True, False), kc, 1)], ["If", Lin], bL, prio)
        if bL != bK:
            il()
        vop(lambda: V.tensor_tensor_scan(u[:, 1:m + 1], T[bK][:, 0:m], T.R1c[:, 0:m], 0.0, A.min, A.max), ["R1c", bK], [nm("u")], m, prio)
        vop(lambda: V.tensor_tensor(kp[:, 0:m], T[bK][:, 0:m], u[:, 0:m], A.is_ge), [bK, nm("u"), nm("u0")], [nm("k")], m, prio)
        if bL == bK:
            il()
        vop(lambda: V.tensor_tensor_scan(re[:, 0:m], T[bP][:, 0:m], kp[:, 0:m], 0.0, A.add, A.mult), [nm("k"), bP], [nm("re")], m, prio)
        for q, (a, z) in enumerate(((0, 16), (16, 24)) if B == 3 else ((0, 8),)):
            vop(lambda a=a, z=z: V.tensor_tensor(e[:, 16 * a:16 * z], re[:, 0:m].indirect(T.oT[:, 24 + a:24 + z]), T.m16[:, 16 * a:16 * z], A.mult),
                [nm("re"), "oE"] + M16, [part("e", q)], 16 * (z - a), prio, f=1.6)
        for b in range(B):
            mm([((T[bL][:, lo + 8 * b:lo + 8 * b + 8], e[:, 128 * b:128 * b + 128], T.Ms[:], False, b == B - 1), 8, 1)],
               [part("e", b // 2), "Ms"], bL, prio)
        if last is not None:
            cp(last[0][:, 0:k], last[1], T[bL][:, lo:lo + k], bL, k, prio)
        else:
            ts(w[:, 0:k], wn, T[bL][:, lo:lo + k], bL, 0.0, float(HI), A.max, A.min, n=k, prio=prio)
            act(L[:, 0:kc], Ln, T[bL][:, lo:lo + kc], [bL], kc, prio)

    ts(T.rk[:, 16:32], "rka", T.L0[:, 0:16], "L0", 10, None, A.arith_shift_right, prio=-4)
    ts(T.rk[:, 0:16], "rkb", T.L0[:, 8:24], "L0", 10, None, A.arith_shift_right, prio=-4)
    RK = ["rka", "rkb"]
    slots(T.oh1, "oh1", 24, 0, CQ, T.rk[:, 0:32], RK, oR, ["oR"], T.Rs[:, 0:168], "Rs", T.su1, "su1", 0)
    ts(T.ti[:], "ti", T.L0[:], "L0", 1023, None, A.bitwise_and, prio=0)
    ts(T.tf[:], "tf", T.ti[:], "ti", 0.5, None, A.add, prio=0)
    pack(T.X[:], "X", T.tf[:], "tf", 24, 0)
    cp(T.W1[:].indirect(T.su1[:]), "W1", T.PK[:], "PK", NP, 0, extra=["su1"], f=3.5)
    decode(T.W1, "W1", T.yi1, "yi1", T.msg1, "msg1", 0)
    s1 = send(T.msg1, "msg1", "hq1", "land1", "rq1", True, 0)

    ts(p8, "p8", pg, "pf", 4.0, p4, A.mult, A.add, n=1, prio=2)
    ts(p32, "p32", pg, "pf", 32.0, p16, A.mult, A.add, n=1, prio=2)
    ts(T.S1[:], "S1", T.S1[:], "S1", p8, None, A.is_equal, n=48, prio=2, extra=["p8"])
    ts(T.sA[:], "sA", T.sA[:], "sA", p32, None, A.is_equal, n=48, prio=2, extra=["p32"])
    ts(T.sC[:, 1:49], "sC", T.sC[:, 1:49], "sC", p32, None, A.is_equal, n=48, prio=2, extra=["p32"])
    fill(T.sC[:, 1:49:6], "sC", 0.0, 8, 2)
    fill(T.sC[:, 6:49:6], "sC", 0.0, 8, 2)
    tt(T.sC[:, 1:49], "sC", T.sA[:], "sA", T.sC[:, 1:49], "sC", A.subtract, n=48, prio=2)
    tt(T.S2[:], "S2", T.sC[:, 0:48], "sC", T.sC[:, 1:49], "sC", A.subtract, n=48, prio=2, extra=["sC0"])
    ts(T.Ms[:], "Ms", T.Ms[:], "Ms", pg, None, A.is_equal, n=8, prio=2, extra=["pf"])
    ts(oE, "oE", T.oKi[:], "oKi", 6.0, 5.0, A.mult, A.add, n=24, prio=2)
    act(T.Rd[:, 0:128], "Rd", T.jm[:], ["jm"], 128, 5)
    ts(T.Rd[:, 0:128], "Rd", T.Rd[:, 0:128], "Rd", 1.0, None, A.min, n=128, prio=5)
    act(T.Rd[:, 128:256], "Rdb", T.Rd[:, 0:128], ["Rd"], 128, 5)
    act(T.Rd[:, 256:384], "Rdc", T.Rd[:, 0:128], ["Rd"], 128, 5)
    ts(T.I1k[:], "I1k", T.I16[:], "I16", 1024.0, None, A.mult, n=64, prio=4)
    gfill(T.scn[:, 56:64], "scnz", 0, 8, 4)
    for t in ("O", "V", "R"):
        gfill(T["u" + t][:, 0:1], "u0" + t, BIG, 1, 2)
    for t in ("V", "R"):
        gfill(T["pr" + t][:, 112:128], "pr" + t, 0, 16, 2)
        gfill(T["pa" + t][:, 112:128], "pa" + t, 0, 16, 2)
    gfill(T.Lv[:, 7:8], "Lv", 0, 1, 2)
    gfill(T.Lv0[:, 7:8], "Lv0", 0, 1, 2)
    cp(T.ND[:], "ND", T.NB[:], "NB", PWID, 2)
    ts(T.Lo[:], "Lo", T.L0[:], "L0", float(-SH) - DEAD, None, A.add, prio=2)
    tt(T.Lo[:], "Lo", T.Lo[:], "Lo", T.oh1[:, 168:192], "oh1", A.mult, prio=2)
    ts(T.Lo[:], "Lo", T.Lo[:], "Lo", DEAD, None, A.add, prio=2)
    ts(T.wO[:], "wO", T.Lo[:], "Lo", 0.0, float(HI), A.max, A.min, prio=2)
    own = lambda pr: step("O", 24, T.X, "X", T.wO, "wO", T.Lo, "Lo", "oK", "oP", "oK", pr)
    own(P_O1)

    def visitors(land, ln, out, outn, sem, sent, fly):
        add("V", lambda: [V.tensor_scalar(T.wv[:, 0:7], land[:, :, 16], 8.0, None, A.add)], [], ["wv", ln], 0.08, 0, [(sem, ARR)], (sent, fly))
        ts(T.Xv[:], "Xv", land[:, :, 0:16], ln, -1024.0, None, A.add, n=112, prio=0)
        add("V", lambda: [V.tensor_scalar(T.Lv0[:, 0:7], land[:, :, 16], 8.0, None, A.add)], [ln], ["Lv0"], 0.08, 1)
        act(T.Lv[:, 0:7], "Lv", T.Lv0[:, 0:7], ["Lv0"], 7, 1)
        a = (7, T.Xv, "Xv", T.wv, "wv", T.Lv, "Lv", "vK", "vP", "vL", 0)
        step("V", *a)
        step("V", *a)
        tt(T.Ld[:], "Ld", T.Lv[:], "Lv", T.Lv0[:], "Lv0", A.subtract, n=8, prio=0)
        step("V", *a, last=(out, outn), Lacc=T.Ld, Laccn="Ld")

    visitors(T.land1, "land1", T.out1, "out1", "rq1", s1, FLY[0])
    s2 = send(T.out1, "out1", "hp1", "rep1", "rp1", False, 0)

    ts(T.sBv[:, 0:7], "sBv", T.yi1[:, :, 16], "yi1t", -DEAD, None, A.add, n=7, prio=4)
    tt(T.sBv[:, 0:7], "sBv", T.sBv[:, 0:7], "sBv", T.cS[:, 0:7], CS[0], A.add, n=7, prio=4, extra=CS[1:])
    ts(T.sBg[:, 0:7], "sBg", T.yi1[:, :, 16], "yi1t", float(NT), None, A.is_lt, n=7, prio=4)
    tt(T.sBv[:, 0:7], "sBv", T.sBv[:, 0:7], "sBv", T.sBg[:, 0:7], "sBg", A.mult, n=7, prio=4)
    ts(T.sBv[:, 0:7], "sBv", T.sBv[:, 0:7], "sBv", DEAD, None, A.add, n=7, prio=4)
    cp(T.yB[:], "yB", T.yi1[:, :, 0:16], "yi1", 112, 4)
    ts(T.xB[:], "xB", T.yi1[:, :, 0:16], "yi1", -1024.0, None, A.add, n=112, prio=5)
    gfill(T.W2[:, 0:112], "W2", NONE, 112, 3)
    gfill(T.Rs[:, 168:224], "RsB", 1, 56, 4)
    gfill(T.Rs[:, 168:224:8], "RsB", 0, 7, 4)
    gfill(T.rkB[:, 7:8], "rkB", rank, 1, 4)
    fill(T.Lb[:, 7:8], "Lb", DEAD, 1, 4)
    ts(T.pj[:, 4:8], "pj4", T.pi[:], "pi", 7, None, A.bitwise_and, n=4, prio=4)
    cp(oB8, "oB8", T.pj[:, 4:8], "pj4", 4, 4)
    own(P_O2)
    own(P_O2)

    RKC = (SH - 511.1875) / 1024.0
    ts(T.rk[:, 16:32], "rka", T.Lo[:, 0:16], "Lo", 1.0 / 1024, RKC, A.mult, A.add, prio=P_A)
    ts(T.rk[:, 0:16], "rkb", T.Lo[:, 8:24], "Lo", 1.0 / 1024, RKC, A.mult, A.add, prio=P_A)
    ts(T.ci[:], "ci", T.Lo[:], "Lo", float(SH), None, A.add, prio=P_A)
    ts(T.ti[:], "ti", T.ci[:], "ci", 1023, None, A.bitwise_and, prio=P_A)
    ts(T.tf[:], "tf", T.ti[:], "ti", 0.5, None, A.add, prio=P_A)
    slots(T.ohA, "ohA", 24, 0, CQ, T.rk[:, 0:32], RK, oR, ["oR"], T.Rs[:, 0:168], "Rs", T.suA, "suA", P_A)
    cp(T.cnt[:, 0:7], "cnt", T.rA[:, 279:424:24], "rA", 7, P_A, extra=["sc"])
    pack(T.X[:], "X", T.tf[:], "tf", 24, P_A)
    cp(T.W2[:].indirect(T.suA[:]), "W2", T.PK[:], "PK", NP, P_A, extra=["suA"], f=3.5)

    vop(lambda: V.tensor_tensor(T.Lb[:, 0:7], T.sBv[:, 0:7], T.rep1[:, 0:7], A.add), ["sBv"], ["Lb"], 7, 0, [("rp1", ARR)], (s2, FLY[1]))
    ts(T.rkB[:, 0:7], "rkB", T.Lb[:, 0:7], "Lb", 1.0 / 1024, RKC, A.mult, A.add, n=7, prio=0)
    ts(T.ci[:, 0:7], "ci", T.Lb[:, 0:7], "Lb", float(SH), None, A.add, n=7, prio=0)
    ts(T.ti[:, 0:7], "ti", T.ci[:, 0:7], "ci", 1023, None, A.bitwise_and, n=7, prio=0)
    slots(T.ohA, "ohA", 8, 192, CQB, T.rkB[:], ["rkB"], oB8, ["oB8"], T.Rs[:, 168:224], "RsB", T.suB, "suB", 0, cnt=T.cnt[:, 0:7])
    pack(T.yB[:], "yB", T.ti[:, 0:8], "ti", 7, 0)
    cp(T.W2[:].indirect(T.suB[:, 0:7]), "W2", T.PK[:, 0:112], "PK", 112, 0, extra=["suB"], f=3.5)
    decode(T.W2, "W2", T.yi2, "yi2", T.msg2, "msg2", 0)
    s3 = send(T.msg2, "msg2", "hq2", "land2", "rq2", True, 0)

    ts(T.wr[:, 0:7], "wr", T.Lb[:, 0:7], "Lb", 0.0, float(HI), A.max, A.min, n=7, prio=P_C)
    cp(T.Gf[:], "Gf", T.G16[:], "G16", 128, P_C)
    gfill(T.vW[:, 112:120], "vW", 0, 8, 4)
    gfill(T.dW[:, 112:136], "dW0", 8192, 24, 4)
    ts(pK, "pK", p16, "pf", 14.5, -float(MID), A.is_lt, A.mult, n=1, prio=5)
    for _ in range(3):
        step("R", 7, T.xB, "xB", T.wr, "wr", T.Lb, "Lb", "rA", "rB", "rC", P_R)
        own(P_O3)
    visitors(T.land2, "land2", T.out2, "out2", "rq2", s3, FLY[2])
    s4 = send(T.out2, "out2", "hp2", "rep2", "rp2", False, 0)

    ts(T.s1c[:], "s1c", T.su1[:], "su1", 112.0, None, A.min, prio=P_C)
    ts(T.smA[:], "smA", T.suA[:], "suA", 128.0, None, A.min, prio=P_C)
    ts(T.smB[:, 0:7], "smB", T.suB[:, 0:7], "suB", 128.0, None, A.min, n=7, prio=P_C)
    ts(T.vB[:, 0:7], "vB", T.Lb[:, 0:7], "Lb", 8192.0, 256.0, A.add, A.mult, n=7, prio=P_C)
    tt(T.vB[:, 0:7], "vB", T.vB[:, 0:7], "vB", T.smB[:, 0:7], "smB", A.add, n=7, prio=P_C)
    vop(lambda: V.tensor_tensor(T.exv[:], T.vB[:, 0:7].indirect(T.oT[:, 0:7]), T.m16[:, 0:112], A.mult), ["vB", "oK"] + M16, ["exv"], 112, P_C, f=1.6)
    mm([((T.rC[:, 0:112], T.Gf[:], T.exv[:], True, True), 112, 1)], ["Gf", "exv"], "rC", P_C)
    cp(T.vW[:, 0:112], "vW", T.rC[:, 0:112], "rC", 112, P_C)
    vop(lambda: V.tensor_tensor(T.gv[:], T.vW[:].indirect(T.s1c[:]), T.m16[:], A.mult), ["vW", "s1c"] + M16, ["gv", "gvb"], NP, P_C, f=1.6)
    vop(lambda: V.tensor_tensor_scan(T.sv[:], T.Rd[:], T.gv[:], 0.0, A.mult, A.add), ["Rd", "Rdb", "Rdc", "gv", "gvb"], ["sv", "svb"], NP, P_C)
    ts(T.vO[:], "vO", T.Lo[:], "Lo", 8192.0, 256.0, A.add, A.mult, prio=P_C)
    tt(T.vO[:], "vO", T.vO[:], "vO", T.smA[:], "smA", A.add, prio=P_C)
    tt(T.vO[:], "vO", T.vO[:], "vO", T.oh1[:, 168:192], "oh1", A.mult, prio=P_C)
    tt(T.vt[:], "vt", T.vO[:], "vO", T.sv[:, 15:NP:16], "sv", A.add, prio=P_C, extra=["svb"])
    ts(T.ci[:], "ci", T.vt[:], "vt", 255, None, A.bitwise_and, prio=P_C)
    cp(T.tau[:], "tau", T.ci[:], "ci", 24, P_C)
    ts(T.vt[:], "vt", T.vt[:], "vt", 8, None, A.arith_shift_right, prio=P_C)
    ts(T.Yb[:], "Yb", T.vt[:], "vt", float(SH - 16384), pK, A.add, A.add, prio=P_C, extra=["pK"])

    vop(lambda: V.tensor_tensor(T.exv[:], T.rep2[:, 0:7].indirect(T.oT[:, 0:7]), T.m16[:, 0:112], A.mult), ["oK"] + M16, ["exv"], 112, 0,
        [("rp2", ARR)], (s4, FLY[3]), f=1.6)
    mm([((T.rC[:, 0:112], T.Gf[:], T.exv[:], True, True), 112, 1)], ["Gf", "exv"], "rC", 0)
    ts(T.dW[:, 0:112], "dW", T.rC[:, 0:112], "rC", 8192.0, None, A.add, n=112, prio=0)
    add("S", lambda: [S.activation(T.gv[:, 192:NP], T.dW[:].indirect(T.tau[:, 12:24]), F.Copy)], ["dW", "dW0", "tau"], ["gvb"], 0.4, 0)
    vop(lambda: V.tensor_copy(T.gv[:, 0:192], T.dW[:].indirect(T.tau[:, 0:12])), ["dW", "dW0", "tau"], ["gv"], 192, 0, f=1.6)
    for h, n in ((0, ""), (192, "b")):
        vop(lambda h=h: V.tensor_tensor_scan(T.sv[:, h:h + 192], T.scC[:], T.gv[:, h:h + 192], 0.0, A.add, A.max), ["scC", "scCb", "gv" + n], ["sv" + n], 192, 0)
    tt(T.vO[:], "vO", T.sv[:, 15:NP:16], "sv", T.Yb[:], "Yb", A.add, prio=0, extra=["svb"])
    load("Y", "st", lambda: [g.sync.dma_start(T.y[:], T.vO[:])], 1, ["vO"], [], 0.1, 0.0)

    order = plan(tasks)
    queue = {"V": V, "S": S, "T": E, "G": g, "Y": g.sync}
    semof = {"V": "sV", "S": "sS", "T": "sT", "G": "sG"}
    done, know, total = {}, {}, {}
    ptr = {q: 0 for q in order}
    known = {q: {} for q in order}
    left = len(tasks)
    while left:
        before = left
        for q in order:
            while ptr[q] < len(order[q]):
                i = order[q][ptr[q]]
                t = tasks[i]
                if any(d not in done for d in t["deps"]):
                    break
                kq = known[q]
                for d in sorted(t["deps"], key=lambda d: (-len(know[d]), -done[d][1])):
                    s, v = done[d]
                    if s is None or kq.get(s, 0) >= v:
                        continue
                    v = max(done[x][1] for x in t["deps"] if done[x][0] == s)
                    if any(done[x][0] not in (s, None) and know[x].get(s, 0) >= v and kq.get(done[x][0], 0) < done[x][1] for x in t["deps"]):
                        continue
                    queue[q].wait_ge(T.sem[s], v)
                    for x in t["deps"]:
                        if done[x][0] == s:
                            for s2, v2 in know[x].items():
                                kq[s2] = max(kq.get(s2, 0), v2)
                    kq[s] = max(kq.get(s, 0), v)
                for s, v in t["ext"]:
                    if kq.get(s, 0) < v:
                        queue[q].wait_ge(T.sem[s], v)
                        kq[s] = v
                ins = t["fn"]()
                if t["dma"]:
                    for x in ins:
                        x.then_inc(T.sem[t["dma"]], 16)
                    done[i] = (t["dma"], loads[t["dma"]])
                elif not ins:
                    done[i] = (None, 0)
                else:
                    s = semof[q]
                    for x in ins:
                        x.then_inc(T.sem[s], 1)
                    total[s] = total.get(s, 0) + len(ins)
                    done[i] = (s, total[s])
                know[i] = dict(kq)
                if done[i][0] is not None:
                    know[i][done[i][0]] = done[i][1]
                ptr[q] += 1
                left -= 1
        if left == before:
            raise ValueError("the order can't be emitted")
    for s, v in sorted(total.items()):
        g.wait_ge(T.sem[s], v)
    for s, v in loads.items():
        g.wait_ge(T.sem[s], v)
    for s in ("rq1", "rp1", "rq2", "rp2"):
        g.wait_ge(T.sem[s], ARR)
    g.wait_ge(T.sem.loc, nloc[0])
